import numpy as np
import ml_dtypes


def mxq(x, axis, fmt="e4m3"):
    dtype, down = {"e4m3": (ml_dtypes.float8_e4m3fn, 7), "e5m2": (ml_dtypes.float8_e5m2, 14)}[fmt]
    v = np.moveaxis(np.asarray(x, np.float32).astype(ml_dtypes.bfloat16).astype(np.float64), axis, -1)
    blocks = v.reshape(v.shape[:-1] + (-1, 32))
    amax = np.abs(blocks).max(-1, keepdims=True)
    byte = np.maximum(np.where(amax > 0, np.frexp(amax)[1] - 1 + 127, 0) - down, 1)
    scale = np.exp2(byte - 127.0)
    codes = (blocks / scale).astype(np.float32).astype(dtype).astype(np.float64)
    return np.moveaxis((codes * scale).reshape(v.shape), -1, axis)


WIDE = False


def mx_kscale(k):
    if not WIDE:
        return np.ones(k)
    levels = np.array([10, -10, 5, -5, 0])
    if k % 512:
        return np.exp2(np.random.permutation(np.resize(levels, k // 32))).repeat(32)
    a = np.empty((k // 512, 16))
    for p in range(k // 512):
        a[p, :8] = np.random.permutation(np.resize(levels, 8))
        for g in range(8):
            far = levels[np.abs(levels - a[p, g]) >= 10]
            a[p, g + 8] = far[np.random.randint(len(far))]
    return np.exp2(a.ravel()).repeat(32)


def f64(x):
    return np.asarray(x).astype(np.float64)


def striped(idx):
    return np.tile(idx.reshape(-1, 16).T, (8, 1)).astype(np.uint16)


def unstriped(offs):
    return offs[:16].T.reshape(-1).astype(np.int64)


E2M1 = np.array([0.0, 0.5, 1.0, 1.5, 2.0, 3.0, 4.0, 6.0, -0.0, -0.5, -1.0, -1.5, -2.0, -3.0, -4.0, -6.0])


def pack_fp4(w):
    k, n = w.shape
    w = f64(np.asarray(w, np.float32).astype(ml_dtypes.bfloat16)).reshape(k // 32, 32, n)
    amax = np.abs(w).max(1)
    mant, ex = np.frexp(amax / 6.0)
    byte = np.clip(np.where(amax > 0, np.where(mant > 0.5, ex, ex - 1) + 127, 1), 1, 254)
    scaled = (w * np.exp2(127.0 - byte)[:, None, :]).reshape(k, n).astype(np.float32)
    c = np.ascontiguousarray(scaled.reshape(k // 512, 128, 4, n).transpose(0, 1, 3, 2)).astype(ml_dtypes.float4_e2m1fn).view(np.uint8) & 0xF
    words = (c[..., 0::2] | (c[..., 1::2] << 4)).reshape(k // 512, 128, 2 * n)
    return np.ascontiguousarray(words), np.ascontiguousarray(byte.astype(np.uint8).reshape(k // 512, 16, n))


def unpack_fp4(words, scales):
    g, _, n = scales.shape
    words = np.ascontiguousarray(words).reshape(g, 128, n, 2)
    nib = np.empty((g, 128, n, 4), np.uint8)
    nib[..., 0::2] = words & 0xF
    nib[..., 1::2] = words >> 4
    vals = E2M1[nib] * np.repeat(np.exp2(scales.astype(np.float64) - 127.0), 8, axis=1)[..., None]
    return vals.transpose(0, 1, 3, 2).reshape(g * 512, n)


def silu(v):
    return v / (1.0 + np.exp(-np.maximum(v, -700.0)))


K, T, S, V, H, N = 512, 2048, 1024, 512, 512, 256


def setup_inputs():
    n = np.random.standard_normal
    s = mx_kscale(K)[:, None]
    u = mx_kscale(H)
    packed_w2 = pack_fp4(n((H, N)) / np.sqrt(3 * H) / u[:, None])
    packed_w3 = pack_fp4(n((H, N)) / np.sqrt(3 * H) / u[:, None])
    packed_w4 = pack_fp4(n((H, N)) / np.sqrt(3 * H) / u[:, None])
    return {
        "xT": (n((K, T)) * s).astype(np.float32),
        "w1": (n((K, H)) / np.sqrt(K) / s * u).astype(np.float32),
        "w2_words": packed_w2[0],
        "w2_scales": packed_w2[1],
        "w3_words": packed_w3[0],
        "w3_scales": packed_w3[1],
        "w4_words": packed_w4[0],
        "w4_scales": packed_w4[1],
        "offs": striped(np.random.permutation(T)[:S]),
        "pos1": striped(np.random.permutation(S)[:V]),
        "pos2": striped(np.random.permutation(S)[:V]),
        "pos3": striped(np.random.permutation(S)[:V]),
        "pos4": striped(np.random.permutation(S)[:V]),
    }


def reference(xT, w1, w2_words, w2_scales, w3_words, w3_scales, w4_words, w4_scales, offs, pos1, pos2, pos3, pos4):
    xq = mxq(f64(xT)[:, unstriped(offs)], 0, "e4m3")
    h = silu(mxq(f64(w1), 0, "e4m3").T @ xq)
    g0 = h[:, unstriped(pos1)]
    g1 = h[:, unstriped(pos2)]
    g2 = h[:, unstriped(pos3)]
    g3 = h[:, unstriped(pos4)]
    z1 = (g0 + g1 + g2 + g3) / 4
    z2 = np.maximum(np.maximum(np.maximum(g0, g1), g2), g3)
    z3 = np.minimum(np.minimum(np.minimum(g0, g1), g2), g3)
    return unpack_fp4(w2_words, w2_scales).T @ mxq(z1, 0, "e4m3") + unpack_fp4(w3_words, w3_scales).T @ mxq(z2, 0, "e4m3") + unpack_fp4(w4_words, w4_scales).T @ mxq(z3, 0, "e4m3")

@@ -1,0 +1,262 @@
+from contextlib import ExitStack
+
+import concourse.mybir as mybir
+from concourse.masks import make_identity
+
+K, T, S, V, H, N = 512, 2048, 1024, 512, 512, 256
+FLOPS = 2 * K * H * S + 3 * 2 * H * N * V
+
+F32 = mybir.dt.float32
+BF16 = mybir.dt.bfloat16
+I32 = mybir.dt.int32
+U32 = mybir.dt.uint32
+U16 = mybir.dt.uint16
+U8 = mybir.dt.uint8
+FP8X4 = mybir.dt.float8_e4m3fn_x4
+FP4X4 = mybir.dt.float4_e2m1fn_x4
+ACT = mybir.ActivationFunctionType
+ALU = mybir.AluOpType
+
+P = 128
+PACK = 4
+DEG = 4
+HALF_S = S // 2
+PART_V = V // 2
+
+
+def tile_picked_pna_silu_e_kernel(
+    tc, xT, w1, w2_words, w2_scales, w3_words, w3_scales, w4_words, w4_scales, offs, pos1, pos2, pos3, pos4, out
+):
+    nc = tc.nc
+    with ExitStack() as ctx:
+        lists = ctx.enter_context(tc.tile_pool(name="lists", bufs=1))
+        keep = ctx.enter_context(tc.tile_pool(name="keep", bufs=1))
+        psum = ctx.enter_context(tc.psum_pool(name="psum", bufs=1))
+
+        def bank(n, shape):
+            return psum.tile(shape, F32, name="bank%d" % n, tag="bank%d" % n)
+
+        zero_in = keep.tile([P, 1], F32, name="zero_in")
+        zero_bias = keep.tile([P, 1], F32, name="zero_bias")
+        nc.vector.memset(zero_in[:], 0.0)
+        nc.scalar.activation(zero_bias[:], zero_in[:], ACT.Silu)
+        ident = keep.tile([P, P], F32, name="ident")
+        make_identity(nc, ident[:])
+        wq_scales = keep.tile([P, 3 * N], U8, name="wq_scales", align_bytes=64)
+        nc.gpsimd.memset(wq_scales[:], 0)
+
+        x_rows = xT.rearrange("(p u e) t -> p u e t", u=2, e=2)
+        x_chunks = [(0, 0, 1024), (0, 1024, 2048), (1, 0, 512), (1, 512, 1024), (1, 1024, 1536), (1, 1536, 2048)]
+        x_raw = []
+        offs_sb = lists.tile([P, S // 16], U16, name="offs_sb")
+        for n, (u, c0, c1) in enumerate(x_chunks):
+            raw = keep.tile([P, 2, c1 - c0], F32, name="x_raw%d" % n)
+            nc.sync.dma_start(out=raw[:], in_=x_rows[:, u, :, c0:c1])
+            x_raw.append(raw)
+            if n == 0:
+                nc.sync.dma_start(offs_sb[:], offs)
+        w_rows = w1.rearrange("(p j) c -> p j c", j=PACK)
+        w_raw = []
+        for n in range(2):
+            raw = keep.tile([P, PACK, H // 2], F32, name="w_raw%d" % n)
+            nc.sync.dma_start(out=raw[:], in_=w_rows[:, :, n * 256 : (n + 1) * 256])
+            w_raw.append(raw)
+        pos_sb = []
+        for d, pos in enumerate((pos1, pos2, pos3, pos4)):
+            tile = lists.tile([P, V // 16], U16, name="pos_sb%d" % d)
+            nc.sync.dma_start(tile[:], pos)
+            pos_sb.append(tile)
+        wq_words = []
+        for a, words in enumerate((w2_words, w3_words, w4_words)):
+            tile = keep.tile([P, 2 * N], U8, name="wq_words%d" % a, align_bytes=64)
+            nc.sync.dma_start(out=tile[:].bitcast(I32), in_=words[0].bitcast(I32))
+            wq_words.append(tile)
+        for a, scales in enumerate((w2_scales, w3_scales, w4_scales)):
+            for q in range(4):
+                nc.sync.dma_start(
+                    out=wq_scales[32 * q : 32 * q + 4, a * N : (a + 1) * N].bitcast(I32),
+                    in_=scales[0, 4 * q : 4 * q + 4, :].bitcast(I32),
+                )
+
+        pairs = [keep.tile([P, T, 2], BF16, name="pairs%d" % u) for u in range(2)]
+        picked = [keep.tile([P, HALF_S, 2], U32, name="picked%d" % s, align_bytes=64) for s in range(2)]
+
+        def cast_x(n, c0, c1, engine):
+            u, base = x_chunks[n][0], x_chunks[n][1]
+            src = x_raw[n][:, :, c0 - base : c1 - base].rearrange("p e t -> p t e")
+            if engine == "vector":
+                nc.vector.tensor_copy(out=pairs[u][:, c0:c1, :], in_=src)
+            else:
+                nc.scalar.copy(out=pairs[u][:, c0:c1, :], in_=src)
+
+        def gather_x(u, s):
+            window = pairs[u][:].rearrange("p t e -> p (t e)").bitcast(U32)
+            nc.vector.tensor_copy(out=picked[s][:, :, u], in_=window.indirect(offs_sb[:, s * 32 : (s + 1) * 32]))
+
+        cast_x(0, 0, 1024, "vector")
+        cast_x(1, 1024, 1408, "scalar")
+        cast_x(1, 1408, 2048, "vector")
+        gather_x(0, 0)
+        gather_x(0, 1)
+        cast_x(2, 0, 512, "scalar")
+        cast_x(3, 512, 1024, "scalar")
+        cast_x(4, 1024, 1536, "scalar")
+        cast_x(5, 1536, 2048, "vector")
+
+        w_grouped = keep.tile([P, PACK, P, PACK], BF16, name="w_grouped", align_bytes=64)
+        for n in range(2):
+            nc.scalar.copy(
+                out=w_grouped[:, :, n * 64 : (n + 1) * 64, :].rearrange("p t m j -> p m j t"),
+                in_=w_raw[n][:].rearrange("p j (m t) -> p m j t", t=PACK),
+            )
+
+        x_codes = [keep.tile([P, HALF_S], U32, name="x_codes%d" % s, align_bytes=64) for s in range(2)]
+        x_scales = [keep.tile([P, HALF_S], U8, name="x_scales%d" % s, align_bytes=64) for s in range(2)]
+        w_codes = keep.tile([P, H], U32, name="w_codes", align_bytes=64)
+        w_scales = keep.tile([P, H], U8, name="w_scales", align_bytes=64)
+
+        def quantize_x(s, c0, c1):
+            nc.vector.quantize_mx(
+                out=x_codes[s][:, c0:c1].bitcast(FP8X4),
+                scales=x_scales[s][:, c0:c1],
+                in_=picked[s][:, c0:c1, :].rearrange("p s u -> p (s u)").bitcast(BF16),
+            )
+
+        def quantize_w(t0, t1):
+            nc.vector.quantize_mx(
+                out=w_codes[:, t0 * P : t1 * P].bitcast(FP8X4),
+                scales=w_scales[:, t0 * P : t1 * P],
+                in_=w_grouped[:, t0:t1].rearrange("p t m j -> p (t m j)"),
+            )
+
+        gather_x(1, 0)
+        gather_x(1, 1)
+        quantize_x(0, 0, 512)
+        quantize_w(0, 1)
+        quantize_x(1, 0, 256)
+        quantize_x(1, 256, 384)
+        quantize_x(1, 384, 512)
+        quantize_w(1, 2)
+        quantize_w(2, 4)
+
+        h_first = keep.tile([P, S], F32, name="h_first")
+        h_rest = keep.tile([P, PACK - 1, S], F32, name="h_rest")
+        h = [h_first[:]] + [h_rest[:, t, :] for t in range(PACK - 1)]
+
+        def product(dst, t, s, c0, c1):
+            nc.tensor.matmul_mx(
+                out=dst,
+                lhsT=w_codes[:, t * P : (t + 1) * P].bitcast(FP8X4),
+                lhsT_scale=w_scales[:, t * P : (t + 1) * P],
+                rhs=x_codes[s][:, c0:c1].bitcast(FP8X4),
+                rhs_scale=x_scales[s][:, c0:c1],
+                start=True,
+                stop=True,
+            )
+
+        def silu(dst, src):
+            nc.scalar.activation(dst, src, ACT.Silu, bias=zero_bias[:])
+
+        turn = 0
+        for t in range(PACK):
+            acc = bank(4 + turn % 4, [P, 512])
+            turn += 1
+            product(acc[:], t, 0, 0, 512)
+            silu(h[t][:, 0:512], acc[:])
+            acc = bank(4 + turn % 4, [P, 384])
+            turn += 1
+            product(acc[:, 0:256], t, 1, 0, 256)
+            product(acc[:, 256:384], t, 1, 256, 384)
+            silu(h[t][:, 512:896], acc[:])
+            if t == 0:
+                acc = bank(4 + turn % 4, [P, P])
+                turn += 1
+                product(acc[:], t, 1, 384, 512)
+                silu(h[t][:, 896:1024], acc[:])
+        acc = bank(4 + turn % 4, [P, PACK - 1, P])
+        for t in range(1, PACK):
+            product(acc[:, t - 1, :], t, 1, 384, 512)
+        silu(h_rest[:, :, 896:1024], acc[:])
+
+        fetched = [keep.tile([P, PACK, V], F32, name="fetched%d" % d) for d in range(DEG)]
+        rounded = [[keep.tile([P, PART_V, PACK], BF16, name="rounded%d_%d" % (d, b)) for b in range(2)] for d in range(DEG)]
+        sum_t = [bank(vb, [P, PACK, P]) for vb in range(V // P)]
+        order = [(0, d) for d in range(DEG)] + [(t, d) for d in range(DEG) for t in range(1, PACK)]
+        for n, (t, d) in enumerate(order):
+            nc.vector.tensor_copy(out=fetched[d][:, t, :], in_=h[t].indirect(pos_sb[d][:]))
+            for vb in range(V // P):
+                nc.tensor.matmul(
+                    sum_t[vb][:, t, :],
+                    lhsT=fetched[d][:, t, vb * P : (vb + 1) * P],
+                    rhs=ident[:],
+                    is_transpose=True,
+                    start=(n == 0),
+                    stop=(n == len(order) - 1),
+                )
+            if t == PACK - 1 and d < DEG - 1:
+                for b in range(2):
+                    nc.scalar.copy(
+                        out=rounded[d][b][:].rearrange("p (c i) t -> p c t i", i=4),
+                        in_=fetched[d][:, :, b * PART_V : (b + 1) * PART_V].rearrange("p t (c i) -> p c t i", i=4),
+                    )
+
+        for b in range(2):
+            d = DEG - 1
+            nc.scalar.copy(
+                out=rounded[d][b][:].rearrange("p (c i) t -> p c t i", i=4),
+                in_=fetched[d][:, :, b * PART_V : (b + 1) * PART_V].rearrange("p t (c i) -> p c t i", i=4),
+            )
+            back = bank(4 + b, [P, 2, PART_V])
+            for r in range(PART_V // P):
+                vb = b * (PART_V // P) + r
+                mean_t = keep.tile([P, 2, P, 2], BF16, name="mean_t%d" % vb)
+                nc.scalar.activation(
+                    mean_t[:], sum_t[vb][:].rearrange("v (u e) p -> v u p e", e=2), ACT.Copy, scale=1.0 / DEG
+                )
+                words = mean_t[:].rearrange("v u p e -> v (u p e)").bitcast(F32)
+                for u in range(2):
+                    nc.tensor.transpose(back[:, u, r * P : (r + 1) * P], words[:, u * P : (u + 1) * P], ident[:])
+            mean = keep.tile([P, PART_V * PACK], BF16, name="mean%d" % b, align_bytes=64)
+            nc.scalar.copy(
+                out=mean[:].bitcast(F32).rearrange("p (v u) -> p v u", u=2), in_=back[:].rearrange("p u v -> p v u")
+            )
+
+            flat = [rounded[d][b][:].rearrange("p v t -> p (v t)") for d in range(DEG)]
+            hi, lo = flat[0], flat[0]
+            for d in range(1, DEG):
+                hi_next = keep.tile([P, PART_V * PACK], BF16, name="hi%d_%d" % (d, b), align_bytes=64)
+                lo_next = keep.tile([P, PART_V * PACK], BF16, name="lo%d_%d" % (d, b), align_bytes=64)
+                nc.vector.tensor_tensor(out=hi_next[:], in0=hi, in1=flat[d], op=ALU.max)
+                nc.vector.tensor_tensor(out=lo_next[:], in0=lo, in1=flat[d], op=ALU.min)
+                hi, lo = hi_next[:], lo_next[:]
+
+            z_codes, z_scales = {}, {}
+            for a, z in ((1, hi), (0, mean[:]), (2, lo)):
+                z_codes[a] = keep.tile([P, PART_V], U32, name="z_codes%d_%d" % (a, b), align_bytes=64)
+                z_scales[a] = keep.tile([P, PART_V], U8, name="z_scales%d_%d" % (a, b), align_bytes=64)
+                nc.vector.quantize_mx(out=z_codes[a][:].bitcast(FP8X4), scales=z_scales[a][:], in_=z)
+
+            res_banks = ((0, 1, 6, 7), (2, 3, 4, 6))[b]
+            res = [bank(n, [P, P]) for n in res_banks]
+            for n, a in enumerate((1, 0, 2)):
+                for m in range(N // P):
+                    for r in range(PART_V // P):
+                        cols = slice(r * P, (r + 1) * P)
+                        nc.tensor.matmul_mx(
+                            out=res[2 * m + r][:],
+                            lhsT=wq_words[a][:, m * 2 * P : (m + 1) * 2 * P].bitcast(FP4X4),
+                            lhsT_scale=wq_scales[:, a * N + m * P : a * N + (m + 1) * P],
+                            rhs=z_codes[a][:, cols].bitcast(FP8X4),
+                            rhs_scale=z_scales[a][:, cols],
+                            start=(n == 0),
+                            stop=(n == 2),
+                        )
+            for m in range(N // P):
+                staged = keep.tile([P, PART_V], F32, name="staged%d_%d" % (m, b))
+                for r in range(PART_V // P):
+                    if b == 1 and m == 1:
+                        nc.vector.tensor_copy(out=staged[:, r * P : (r + 1) * P], in_=res[2 * m + r][:])
+                    else:
+                        nc.scalar.copy(out=staged[:, r * P : (r + 1) * P], in_=res[2 * m + r][:])
+                queue = nc.scalar if (b == 1 and m == 0) else nc.sync
+                queue.dma_start(out=out[m * P : (m + 1) * P, b * PART_V : (b + 1) * PART_V], in_=staged[:])

@@ -20,8 +20,15 @@ ALU = mybir.AluOpType
 P = 128
 PACK = 4
 DEG = 4
+PER_COLUMN = 16
 HALF_S = S // 2
-PART_V = V // 2
+QUARTER_S = S // 4
+HALF_V = V // 2
+MEAN, LARGEST, SMALLEST = 0, 1, 2
+
+X_LOADS = ((0, 0, 1280), (0, 1280, 2048), (1, 0, 1024), (1, 1024, 1664), (1, 1664, 2048))
+SCALAR_SHARE = 3
+LATE_PIECES = ((0, 256), (256, 384), (384, 512))
 
 
 def tile_picked_pna_silu_e_kernel(
@@ -46,72 +53,91 @@ def tile_picked_pna_silu_e_kernel(
         nc.gpsimd.memset(wq_scales[:], 0)
 
         x_rows = xT.rearrange("(p u e) t -> p u e t", u=2, e=2)
-        x_chunks = [(0, 0, 1024), (0, 1024, 2048), (1, 0, 512), (1, 512, 1024), (1, 1024, 1536), (1, 1536, 2048)]
         x_raw = []
-        offs_sb = lists.tile([P, S // 16], U16, name="offs_sb")
-        for n, (u, c0, c1) in enumerate(x_chunks):
+        offs_sb = lists.tile([P, S // PER_COLUMN], U16, name="offs_sb")
+        for n, (u, c0, c1) in enumerate(X_LOADS):
             raw = keep.tile([P, 2, c1 - c0], F32, name="x_raw%d" % n)
             nc.sync.dma_start(out=raw[:], in_=x_rows[:, u, :, c0:c1])
             x_raw.append(raw)
             if n == 0:
                 nc.sync.dma_start(offs_sb[:], offs)
-        w_rows = w1.rearrange("(p j) c -> p j c", j=PACK)
-        w_raw = []
-        for n in range(2):
-            raw = keep.tile([P, PACK, H // 2], F32, name="w_raw%d" % n)
-            nc.sync.dma_start(out=raw[:], in_=w_rows[:, :, n * 256 : (n + 1) * 256])
-            w_raw.append(raw)
+        w_raw = keep.tile([P, PACK, H], F32, name="w_raw")
+        nc.sync.dma_start(out=w_raw[:], in_=w1.rearrange("(p j) c -> p j c", j=PACK))
         pos_sb = []
         for d, pos in enumerate((pos1, pos2, pos3, pos4)):
-            tile = lists.tile([P, V // 16], U16, name="pos_sb%d" % d)
-            nc.sync.dma_start(tile[:], pos)
-            pos_sb.append(tile)
+            pos_tile = lists.tile([P, V // PER_COLUMN], U16, name="pos_sb%d" % d)
+            nc.sync.dma_start(pos_tile[:], pos)
+            pos_sb.append(pos_tile)
         wq_words = []
-        for a, words in enumerate((w2_words, w3_words, w4_words)):
-            tile = keep.tile([P, 2 * N], U8, name="wq_words%d" % a, align_bytes=64)
-            nc.sync.dma_start(out=tile[:].bitcast(I32), in_=words[0].bitcast(I32))
-            wq_words.append(tile)
-        for a, scales in enumerate((w2_scales, w3_scales, w4_scales)):
+        for a, words_hbm in enumerate((w2_words, w3_words, w4_words)):
+            words_tile = keep.tile([P, 2 * N], U8, name="wq_words%d" % a, align_bytes=64)
+            nc.sync.dma_start(out=words_tile[:].bitcast(I32), in_=words_hbm[0].bitcast(I32))
+            wq_words.append(words_tile)
+        for a, scales_hbm in enumerate((w2_scales, w3_scales, w4_scales)):
             for q in range(4):
                 nc.sync.dma_start(
                     out=wq_scales[32 * q : 32 * q + 4, a * N : (a + 1) * N].bitcast(I32),
-                    in_=scales[0, 4 * q : 4 * q + 4, :].bitcast(I32),
+                    in_=scales_hbm[0, 4 * q : 4 * q + 4, :].bitcast(I32),
                 )
 
         pairs = [keep.tile([P, T, 2], BF16, name="pairs%d" % u) for u in range(2)]
-        picked = [keep.tile([P, HALF_S, 2], U32, name="picked%d" % s, align_bytes=64) for s in range(2)]
+        picked_pair = [keep.tile([P, 2, HALF_S], I32, name="picked_pair%d" % s) for s in range(2)]
+        picked = [
+            keep.tile([P, HALF_S, 2], I32, name="picked%d" % s, tag="picked%d" % s, align_bytes=64) for s in range(2)
+        ]
 
-        def cast_x(n, c0, c1, engine):
-            u, base = x_chunks[n][0], x_chunks[n][1]
-            src = x_raw[n][:, :, c0 - base : c1 - base].rearrange("p e t -> p t e")
-            if engine == "vector":
-                nc.vector.tensor_copy(out=pairs[u][:, c0:c1, :], in_=src)
-            else:
-                nc.scalar.copy(out=pairs[u][:, c0:c1, :], in_=src)
-
-        def gather_x(u, s):
-            window = pairs[u][:].rearrange("p t e -> p (t e)").bitcast(U32)
-            nc.vector.tensor_copy(out=picked[s][:, :, u], in_=window.indirect(offs_sb[:, s * 32 : (s + 1) * 32]))
-
-        cast_x(0, 0, 1024, "vector")
-        cast_x(1, 1024, 1408, "scalar")
-        cast_x(1, 1408, 2048, "vector")
-        gather_x(0, 0)
-        gather_x(0, 1)
-        cast_x(2, 0, 512, "scalar")
-        cast_x(3, 512, 1024, "scalar")
-        cast_x(4, 1024, 1536, "scalar")
-        cast_x(5, 1536, 2048, "vector")
-
-        w_grouped = keep.tile([P, PACK, P, PACK], BF16, name="w_grouped", align_bytes=64)
-        for n in range(2):
-            nc.scalar.copy(
-                out=w_grouped[:, :, n * 64 : (n + 1) * 64, :].rearrange("p t m j -> p m j t"),
-                in_=w_raw[n][:].rearrange("p j (m t) -> p m j t", t=PACK),
+        def round_x(n, c0, c1, copy):
+            u, base = X_LOADS[n][0], X_LOADS[n][1]
+            copy(
+                out=pairs[u][:, c0:c1, :].rearrange("p (c i) e -> p c e i", i=4),
+                in_=x_raw[n][:, :, c0 - base : c1 - base].rearrange("p e (c i) -> p c e i", i=4),
             )
 
-        x_codes = [keep.tile([P, HALF_S], U32, name="x_codes%d" % s, align_bytes=64) for s in range(2)]
-        x_scales = [keep.tile([P, HALF_S], U8, name="x_scales%d" % s, align_bytes=64) for s in range(2)]
+        def round_x_shared(n):
+            c0, c1 = X_LOADS[n][1], X_LOADS[n][2]
+            cut = c0 + (c1 - c0) // SCALAR_SHARE
+            round_x(n, c0, cut, nc.scalar.copy)
+            round_x(n, cut, c1, nc.vector.tensor_copy)
+
+        def gather_x(u, s, c0, c1):
+            window = pairs[u][:].rearrange("p t e -> p (t e)").bitcast(U32)
+            offsets = offs_sb[:, (s * HALF_S + c0) // PER_COLUMN : (s * HALF_S + c1) // PER_COLUMN]
+            nc.vector.tensor_copy(out=picked_pair[s][:, u, c0:c1].bitcast(U32), in_=window.indirect(offsets))
+
+        def weave_views(s, c0, c1):
+            dst = picked[s][:, c0:c1, :].rearrange("p (c i) u -> p c u i", i=2)
+            src = picked_pair[s][:, :, c0:c1].rearrange("p u (c i) -> p c u i", i=2)
+            return dst, src
+
+        round_x(0, X_LOADS[0][1], X_LOADS[0][2], nc.vector.tensor_copy)
+        round_x_shared(1)
+        for s in range(2):
+            gather_x(0, s, 0, HALF_S)
+        round_x(2, X_LOADS[2][1], X_LOADS[2][2], nc.scalar.copy)
+        round_x(3, X_LOADS[3][1], X_LOADS[3][2], nc.vector.tensor_copy)
+        round_x_shared(4)
+        for s in range(2):
+            for c0 in range(0, HALF_S, QUARTER_S):
+                gather_x(1, s, c0, c0 + QUARTER_S)
+        for c0 in range(0, HALF_S, QUARTER_S):
+            dst, src = weave_views(0, c0, c0 + QUARTER_S)
+            nc.scalar.copy(out=dst.bitcast(U32), in_=src.bitcast(U32))
+        for c0 in range(0, HALF_S, QUARTER_S):
+            dst, src = weave_views(1, c0, c0 + QUARTER_S)
+            nc.vector.tensor_copy(out=dst, in_=src)
+
+        w_grouped = [
+            keep.tile([P, 2, P, PACK], BF16, name="w_grouped%d" % g, tag="w_grouped%d" % g, align_bytes=64)
+            for g in range(2)
+        ]
+        for g in range(2):
+            nc.scalar.copy(
+                out=w_grouped[g][:].rearrange("p e m j -> p m j e"),
+                in_=w_raw[:].rearrange("p j (m t) -> p m j t", t=PACK)[:, :, :, 2 * g : 2 * g + 2],
+            )
+
+        x_codes = [keep.tile([P, HALF_S], U32, name="x_codes0", align_bytes=64)]
+        x_scales = [keep.tile([P, HALF_S], U8, name="x_scales0", align_bytes=64)]
         w_codes = keep.tile([P, H], U32, name="w_codes", align_bytes=64)
         w_scales = keep.tile([P, H], U8, name="w_scales", align_bytes=64)
 
@@ -122,22 +148,20 @@ def tile_picked_pna_silu_e_kernel(
                 in_=picked[s][:, c0:c1, :].rearrange("p s u -> p (s u)").bitcast(BF16),
             )
 
-        def quantize_w(t0, t1):
+        def quantize_w(g):
             nc.vector.quantize_mx(
-                out=w_codes[:, t0 * P : t1 * P].bitcast(FP8X4),
-                scales=w_scales[:, t0 * P : t1 * P],
-                in_=w_grouped[:, t0:t1].rearrange("p t m j -> p (t m j)"),
+                out=w_codes[:, 2 * g * P : 2 * (g + 1) * P].bitcast(FP8X4),
+                scales=w_scales[:, 2 * g * P : 2 * (g + 1) * P],
+                in_=w_grouped[g][:].rearrange("p e m j -> p (e m j)"),
             )
 
-        gather_x(1, 0)
-        gather_x(1, 1)
-        quantize_x(0, 0, 512)
-        quantize_w(0, 1)
-        quantize_x(1, 0, 256)
-        quantize_x(1, 256, 384)
-        quantize_x(1, 384, 512)
-        quantize_w(1, 2)
-        quantize_w(2, 4)
+        quantize_x(0, 0, HALF_S)
+        quantize_w(0)
+        x_codes.append(keep.tile([P, HALF_S], U32, name="x_codes1", tag="picked0", align_bytes=64))
+        x_scales.append(keep.tile([P, HALF_S], U8, name="x_scales1", tag="w_grouped0", align_bytes=64))
+        for c0, c1 in LATE_PIECES:
+            quantize_x(1, c0, c1)
+        quantize_w(1)
 
         h_first = keep.tile([P, S], F32, name="h_first")
         h_rest = keep.tile([P, PACK - 1, S], F32, name="h_rest")
@@ -157,29 +181,36 @@ def tile_picked_pna_silu_e_kernel(
         def silu(dst, src):
             nc.scalar.activation(dst, src, ACT.Silu, bias=zero_bias[:])
 
-        turn = 0
-        for t in range(PACK):
-            acc = bank(4 + turn % 4, [P, 512])
-            turn += 1
-            product(acc[:], t, 0, 0, 512)
-            silu(h[t][:, 0:512], acc[:])
-            acc = bank(4 + turn % 4, [P, 384])
-            turn += 1
-            product(acc[:, 0:256], t, 1, 0, 256)
-            product(acc[:, 256:384], t, 1, 256, 384)
-            silu(h[t][:, 512:896], acc[:])
-            if t == 0:
-                acc = bank(4 + turn % 4, [P, P])
-                turn += 1
-                product(acc[:], t, 1, 384, 512)
-                silu(h[t][:, 896:1024], acc[:])
-        acc = bank(4 + turn % 4, [P, PACK - 1, P])
+        acc = bank(4, [P, HALF_S])
+        product(acc[:], 0, 0, 0, HALF_S)
+        silu(h[0][:, 0:HALF_S], acc[:])
+        for n, (c0, c1) in enumerate(LATE_PIECES):
+            acc = bank(5 + n, [P, c1 - c0])
+            product(acc[:], 0, 1, c0, c1)
+            silu(h[0][:, HALF_S + c0 : HALF_S + c1], acc[:])
+        last0, last1 = LATE_PIECES[-1]
         for t in range(1, PACK):
-            product(acc[:, t - 1, :], t, 1, 384, 512)
-        silu(h_rest[:, :, 896:1024], acc[:])
+            acc = bank(4 + (2 * t) % 4, [P, HALF_S])
+            product(acc[:], t, 0, 0, HALF_S)
+            silu(h[t][:, 0:HALF_S], acc[:])
+            acc = bank(4 + (2 * t + 1) % 4, [P, last0])
+            for c0, c1 in LATE_PIECES[:-1]:
+                product(acc[:, c0:c1], t, 1, c0, c1)
+            silu(h[t][:, HALF_S : HALF_S + last0], acc[:])
+        acc = bank(4, [P, PACK - 1, last1 - last0])
+        for t in range(1, PACK):
+            product(acc[:, t - 1, :], t, 1, last0, last1)
+        silu(h_rest[:, :, HALF_S + last0 : HALF_S + last1], acc[:])
 
         fetched = [keep.tile([P, PACK, V], F32, name="fetched%d" % d) for d in range(DEG)]
-        rounded = [[keep.tile([P, PART_V, PACK], BF16, name="rounded%d_%d" % (d, b)) for b in range(2)] for d in range(DEG)]
+        rounded = [keep.tile([P, V, PACK], BF16, name="rounded%d" % d) for d in range(DEG)]
+
+        def round_fetched(d, v0, v1):
+            nc.scalar.copy(
+                out=rounded[d][:, v0:v1, :].rearrange("p (c i) t -> p c t i", i=4),
+                in_=fetched[d][:, :, v0:v1].rearrange("p t (c i) -> p c t i", i=4),
+            )
+
         sum_t = [bank(vb, [P, PACK, P]) for vb in range(V // P)]
         order = [(0, d) for d in range(DEG)] + [(t, d) for d in range(DEG) for t in range(1, PACK)]
         for n, (t, d) in enumerate(order):
@@ -194,69 +225,81 @@ def tile_picked_pna_silu_e_kernel(
                     stop=(n == len(order) - 1),
                 )
             if t == PACK - 1 and d < DEG - 1:
-                for b in range(2):
-                    nc.scalar.copy(
-                        out=rounded[d][b][:].rearrange("p (c i) t -> p c t i", i=4),
-                        in_=fetched[d][:, :, b * PART_V : (b + 1) * PART_V].rearrange("p t (c i) -> p c t i", i=4),
-                    )
+                round_fetched(d, 0, V)
 
-        for b in range(2):
-            d = DEG - 1
-            nc.scalar.copy(
-                out=rounded[d][b][:].rearrange("p (c i) t -> p c t i", i=4),
-                in_=fetched[d][:, :, b * PART_V : (b + 1) * PART_V].rearrange("p t (c i) -> p c t i", i=4),
-            )
-            back = bank(4 + b, [P, 2, PART_V])
-            for r in range(PART_V // P):
-                vb = b * (PART_V // P) + r
+        flat = [rounded[d][:].rearrange("p v t -> p (v t)") for d in range(DEG)]
+        hi_run, lo_run = flat[0], flat[0]
+        for d in range(1, DEG - 1):
+            hi_next = keep.tile([P, V * PACK], BF16, name="hi%d" % d)
+            lo_next = keep.tile([P, V * PACK], BF16, name="lo%d" % d)
+            nc.vector.tensor_tensor(out=hi_next[:], in0=hi_run, in1=flat[d], op=ALU.max)
+            nc.vector.tensor_tensor(out=lo_next[:], in0=lo_run, in1=flat[d], op=ALU.min)
+            hi_run, lo_run = hi_next[:], lo_next[:]
+
+        blocks = HALF_V // P
+        for half in range(2):
+            round_fetched(DEG - 1, half * HALF_V, (half + 1) * HALF_V)
+
+            back = bank(4 + half, [P, 2, HALF_V])
+            for r in range(blocks):
+                vb = half * blocks + r
                 mean_t = keep.tile([P, 2, P, 2], BF16, name="mean_t%d" % vb)
                 nc.scalar.activation(
                     mean_t[:], sum_t[vb][:].rearrange("v (u e) p -> v u p e", e=2), ACT.Copy, scale=1.0 / DEG
                 )
-                words = mean_t[:].rearrange("v u p e -> v (u p e)").bitcast(F32)
+                mean_words = mean_t[:].rearrange("v u p e -> v (u p e)").bitcast(F32)
                 for u in range(2):
-                    nc.tensor.transpose(back[:, u, r * P : (r + 1) * P], words[:, u * P : (u + 1) * P], ident[:])
-            mean = keep.tile([P, PART_V * PACK], BF16, name="mean%d" % b, align_bytes=64)
-            nc.scalar.copy(
-                out=mean[:].bitcast(F32).rearrange("p (v u) -> p v u", u=2), in_=back[:].rearrange("p u v -> p v u")
-            )
+                    nc.tensor.transpose(back[:, u, r * P : (r + 1) * P], mean_words[:, u * P : (u + 1) * P], ident[:])
+            mean = []
+            for r in range(blocks):
+                mean_name = "mean%d_%d" % (half, r)
+                mean_block = keep.tile([P, P * PACK], BF16, name=mean_name, tag=mean_name, align_bytes=64)
+                nc.scalar.copy(
+                    out=mean_block[:].bitcast(F32).rearrange("p (v u) -> p v u", u=2),
+                    in_=back[:, :, r * P : (r + 1) * P].rearrange("p u v -> p v u"),
+                )
+                mean.append(mean_block[:])
 
-            flat = [rounded[d][b][:].rearrange("p v t -> p (v t)") for d in range(DEG)]
-            hi, lo = flat[0], flat[0]
-            for d in range(1, DEG):
-                hi_next = keep.tile([P, PART_V * PACK], BF16, name="hi%d_%d" % (d, b), align_bytes=64)
-                lo_next = keep.tile([P, PART_V * PACK], BF16, name="lo%d_%d" % (d, b), align_bytes=64)
-                nc.vector.tensor_tensor(out=hi_next[:], in0=hi, in1=flat[d], op=ALU.max)
-                nc.vector.tensor_tensor(out=lo_next[:], in0=lo, in1=flat[d], op=ALU.min)
-                hi, lo = hi_next[:], lo_next[:]
+            cols = slice(half * HALF_V * PACK, (half + 1) * HALF_V * PACK)
+            extremes = keep.tile(
+                [P, 2, HALF_V * PACK], BF16, name="extremes%d" % half, tag=("extremes0", "mean0_0")[half], align_bytes=64
+            )
+            hi, lo = extremes[:, 0, :], extremes[:, 1, :]
+            nc.vector.tensor_tensor(out=hi, in0=hi_run[:, cols], in1=flat[DEG - 1][:, cols], op=ALU.max)
+            nc.vector.tensor_tensor(out=lo, in0=lo_run[:, cols], in1=flat[DEG - 1][:, cols], op=ALU.min)
 
             z_codes, z_scales = {}, {}
-            for a, z in ((1, hi), (0, mean[:]), (2, lo)):
-                z_codes[a] = keep.tile([P, PART_V], U32, name="z_codes%d_%d" % (a, b), align_bytes=64)
-                z_scales[a] = keep.tile([P, PART_V], U8, name="z_scales%d_%d" % (a, b), align_bytes=64)
-                nc.vector.quantize_mx(out=z_codes[a][:].bitcast(FP8X4), scales=z_scales[a][:], in_=z)
+            for a, pieces in ((LARGEST, [hi]), (SMALLEST, [lo]), (MEAN, mean)):
+                width = HALF_V // len(pieces)
+                z_codes[a] = keep.tile([P, HALF_V], U32, name="z_codes%d_%d" % (a, half), align_bytes=64)
+                z_scales[a] = keep.tile([P, HALF_V], U8, name="z_scales%d_%d" % (a, half), align_bytes=64)
+                for n, z in enumerate(pieces):
+                    nc.vector.quantize_mx(
+                        out=z_codes[a][:, n * width : (n + 1) * width].bitcast(FP8X4),
+                        scales=z_scales[a][:, n * width : (n + 1) * width],
+                        in_=z,
+                    )
 
-            res_banks = ((0, 1, 6, 7), (2, 3, 4, 6))[b]
+            res_banks = ((0, 1, 6, 7), (2, 3, 4, 6))[half]
             res = [bank(n, [P, P]) for n in res_banks]
-            for n, a in enumerate((1, 0, 2)):
-                for m in range(N // P):
-                    for r in range(PART_V // P):
-                        cols = slice(r * P, (r + 1) * P)
+            for n, a in enumerate((LARGEST, SMALLEST, MEAN)):
+                for r in range(blocks):
+                    for m in range(N // P):
                         nc.tensor.matmul_mx(
-                            out=res[2 * m + r][:],
+                            out=res[blocks * m + r][:],
                             lhsT=wq_words[a][:, m * 2 * P : (m + 1) * 2 * P].bitcast(FP4X4),
                             lhsT_scale=wq_scales[:, a * N + m * P : a * N + (m + 1) * P],
-                            rhs=z_codes[a][:, cols].bitcast(FP8X4),
-                            rhs_scale=z_scales[a][:, cols],
+                            rhs=z_codes[a][:, r * P : (r + 1) * P].bitcast(FP8X4),
+                            rhs_scale=z_scales[a][:, r * P : (r + 1) * P],
                             start=(n == 0),
                             stop=(n == 2),
                         )
+            staged = [keep.tile([P, HALF_V], F32, name="staged%d_%d" % (m, half)) for m in range(N // P)]
+            for r in range(blocks):
+                for m in range(N // P):
+                    very_last = half == 1 and r == blocks - 1 and m == N // P - 1
+                    copy = nc.vector.tensor_copy if very_last else nc.scalar.copy
+                    copy(out=staged[m][:, r * P : (r + 1) * P], in_=res[blocks * m + r][:])
             for m in range(N // P):
-                staged = keep.tile([P, PART_V], F32, name="staged%d_%d" % (m, b))
-                for r in range(PART_V // P):
-                    if b == 1 and m == 1:
-                        nc.vector.tensor_copy(out=staged[:, r * P : (r + 1) * P], in_=res[2 * m + r][:])
-                    else:
-                        nc.scalar.copy(out=staged[:, r * P : (r + 1) * P], in_=res[2 * m + r][:])
-                queue = nc.scalar if (b == 1 and m == 0) else nc.sync
-                queue.dma_start(out=out[m * P : (m + 1) * P, b * PART_V : (b + 1) * PART_V], in_=staged[:])
+                queue = nc.scalar if (half == 1 and m == 0) else nc.sync
+                queue.dma_start(out=out[m * P : (m + 1) * P, half * HALF_V : (half + 1) * HALF_V], in_=staged[m][:])

@@ -26,9 +26,9 @@ QUARTER_S = S // 4
 HALF_V = V // 2
 MEAN, LARGEST, SMALLEST = 0, 1, 2
 
-X_LOADS = ((0, 0, 1280), (0, 1280, 2048), (1, 0, 1024), (1, 1024, 1664), (1, 1664, 2048))
-SCALAR_SHARE = 3
-LATE_PIECES = ((0, 256), (256, 384), (384, 512))
+X_LOADS = ((0, 0, 1280, 0), (0, 1280, 2048, 384), (1, 0, 1024, 640), (1, 1024, 1792, 256), (1, 1792, 2048, 64))
+PIECES = ((0, 256), (256, 512), (512, 768), (768, 896), (896, 1024))
+W_LOADS = 2
 
 
 def tile_picked_pna_silu_e_kernel(
@@ -55,14 +55,19 @@ def tile_picked_pna_silu_e_kernel(
         x_rows = xT.rearrange("(p u e) t -> p u e t", u=2, e=2)
         x_raw = []
         offs_sb = lists.tile([P, S // PER_COLUMN], U16, name="offs_sb")
-        for n, (u, c0, c1) in enumerate(X_LOADS):
+        for n, (u, c0, c1, share) in enumerate(X_LOADS):
             raw = keep.tile([P, 2, c1 - c0], F32, name="x_raw%d" % n)
             nc.sync.dma_start(out=raw[:], in_=x_rows[:, u, :, c0:c1])
             x_raw.append(raw)
             if n == 0:
                 nc.sync.dma_start(offs_sb[:], offs)
-        w_raw = keep.tile([P, PACK, H], F32, name="w_raw")
-        nc.sync.dma_start(out=w_raw[:], in_=w1.rearrange("(p j) c -> p j c", j=PACK))
+        w_rows = w1.rearrange("(p j) c -> p j c", j=PACK)
+        w_width = H // W_LOADS
+        w_raw = []
+        for n in range(W_LOADS):
+            raw = keep.tile([P, PACK, w_width], F32, name="w_raw%d" % n, tag="w_raw%d" % n)
+            nc.sync.dma_start(out=raw[:], in_=w_rows[:, :, n * w_width : (n + 1) * w_width])
+            w_raw.append(raw)
         pos_sb = []
         for d, pos in enumerate((pos1, pos2, pos3, pos4)):
             pos_tile = lists.tile([P, V // PER_COLUMN], U16, name="pos_sb%d" % d)
@@ -81,71 +86,65 @@ def tile_picked_pna_silu_e_kernel(
                 )
 
         pairs = [keep.tile([P, T, 2], BF16, name="pairs%d" % u) for u in range(2)]
-        picked_pair = [keep.tile([P, 2, HALF_S], I32, name="picked_pair%d" % s) for s in range(2)]
-        picked = [
-            keep.tile([P, HALF_S, 2], I32, name="picked%d" % s, tag="picked%d" % s, align_bytes=64) for s in range(2)
-        ]
+        picked_pair = keep.tile([P, 2, S], I32, name="picked_pair")
+        woven = [keep.tile([P, QUARTER_S, 2], I32, name="woven%d" % q, align_bytes=64) for q in range(4)]
 
-        def round_x(n, c0, c1, copy):
-            u, base = X_LOADS[n][0], X_LOADS[n][1]
-            copy(
-                out=pairs[u][:, c0:c1, :].rearrange("p (c i) e -> p c e i", i=4),
-                in_=x_raw[n][:, :, c0 - base : c1 - base].rearrange("p e (c i) -> p c e i", i=4),
-            )
+        def round_x(n):
+            u, c0, c1, share = X_LOADS[n]
+            for a, b, copy in ((0, share, nc.scalar.copy), (share, c1 - c0, nc.vector.tensor_copy)):
+                if b > a:
+                    copy(
+                        out=pairs[u][:, c0 + a : c0 + b, :].rearrange("p (c i) e -> p c e i", i=4),
+                        in_=x_raw[n][:, :, a:b].rearrange("p e (c i) -> p c e i", i=4),
+                    )
 
-        def round_x_shared(n):
-            c0, c1 = X_LOADS[n][1], X_LOADS[n][2]
-            cut = c0 + (c1 - c0) // SCALAR_SHARE
-            round_x(n, c0, cut, nc.scalar.copy)
-            round_x(n, cut, c1, nc.vector.tensor_copy)
-
-        def gather_x(u, s, c0, c1):
+        def gather_x(dst, u, c0, c1):
             window = pairs[u][:].rearrange("p t e -> p (t e)").bitcast(U32)
-            offsets = offs_sb[:, (s * HALF_S + c0) // PER_COLUMN : (s * HALF_S + c1) // PER_COLUMN]
-            nc.vector.tensor_copy(out=picked_pair[s][:, u, c0:c1].bitcast(U32), in_=window.indirect(offsets))
+            offsets = offs_sb[:, c0 // PER_COLUMN : c1 // PER_COLUMN]
+            nc.vector.tensor_copy(out=dst.bitcast(U32), in_=window.indirect(offsets))
 
-        def weave_views(s, c0, c1):
-            dst = picked[s][:, c0:c1, :].rearrange("p (c i) u -> p c u i", i=2)
-            src = picked_pair[s][:, :, c0:c1].rearrange("p u (c i) -> p c u i", i=2)
-            return dst, src
-
-        round_x(0, X_LOADS[0][1], X_LOADS[0][2], nc.vector.tensor_copy)
-        round_x_shared(1)
-        for s in range(2):
-            gather_x(0, s, 0, HALF_S)
-        round_x(2, X_LOADS[2][1], X_LOADS[2][2], nc.scalar.copy)
-        round_x(3, X_LOADS[3][1], X_LOADS[3][2], nc.vector.tensor_copy)
-        round_x_shared(4)
-        for s in range(2):
-            for c0 in range(0, HALF_S, QUARTER_S):
-                gather_x(1, s, c0, c0 + QUARTER_S)
-        for c0 in range(0, HALF_S, QUARTER_S):
-            dst, src = weave_views(0, c0, c0 + QUARTER_S)
-            nc.scalar.copy(out=dst.bitcast(U32), in_=src.bitcast(U32))
-        for c0 in range(0, HALF_S, QUARTER_S):
-            dst, src = weave_views(1, c0, c0 + QUARTER_S)
-            nc.vector.tensor_copy(out=dst, in_=src)
+        round_x(0)
+        round_x(1)
+        gather_x(picked_pair[:, 0, :], 0, 0, S)
+        for n in range(2, len(X_LOADS)):
+            round_x(n)
+        for q in range(4):
+            cols = slice(q * QUARTER_S, (q + 1) * QUARTER_S)
+            gather_x(picked_pair[:, 1, cols], 1, cols.start, cols.stop)
+            nc.scalar.copy(
+                out=woven[q][:].rearrange("p (c i) u -> p c u i", i=2).bitcast(U32),
+                in_=picked_pair[:, :, cols].rearrange("p u (c i) -> p c u i", i=2).bitcast(U32),
+            )
 
         w_grouped = [
             keep.tile([P, 2, P, PACK], BF16, name="w_grouped%d" % g, tag="w_grouped%d" % g, align_bytes=64)
             for g in range(2)
         ]
-        for g in range(2):
-            nc.scalar.copy(
-                out=w_grouped[g][:].rearrange("p e m j -> p m j e"),
-                in_=w_raw[:].rearrange("p j (m t) -> p m j t", t=PACK)[:, :, :, 2 * g : 2 * g + 2],
+
+        def group_w(g, n, copy):
+            m_width = P // W_LOADS
+            copy(
+                out=w_grouped[g][:, :, n * m_width : (n + 1) * m_width, :].rearrange("p e m j -> p m j e"),
+                in_=w_raw[n][:].rearrange("p j (m t) -> p m j t", t=PACK)[:, :, :, 2 * g : 2 * g + 2],
             )
 
-        x_codes = [keep.tile([P, HALF_S], U32, name="x_codes0", align_bytes=64)]
-        x_scales = [keep.tile([P, HALF_S], U8, name="x_scales0", align_bytes=64)]
+        group_w(0, 0, nc.vector.tensor_copy)
+        group_w(0, 1, nc.vector.tensor_copy)
+        group_w(1, 0, nc.scalar.copy)
+
+        x_codes = keep.tile([P, S], U32, name="x_codes", align_bytes=64)
         w_codes = keep.tile([P, H], U32, name="w_codes", align_bytes=64)
         w_scales = keep.tile([P, H], U8, name="w_scales", align_bytes=64)
+        x_scales = []
 
-        def quantize_x(s, c0, c1):
+        def quantize_x(n):
+            c0, c1 = PIECES[n]
+            q = c0 // QUARTER_S
+            src = woven[q][:, c0 - q * QUARTER_S : c1 - q * QUARTER_S, :]
             nc.vector.quantize_mx(
-                out=x_codes[s][:, c0:c1].bitcast(FP8X4),
-                scales=x_scales[s][:, c0:c1],
-                in_=picked[s][:, c0:c1, :].rearrange("p s u -> p (s u)").bitcast(BF16),
+                out=x_codes[:, c0:c1].bitcast(FP8X4),
+                scales=x_scales[n],
+                in_=src.rearrange("p s u -> p (s u)").bitcast(BF16),
             )
 
         def quantize_w(g):
@@ -155,25 +154,29 @@ def tile_picked_pna_silu_e_kernel(
                 in_=w_grouped[g][:].rearrange("p e m j -> p (e m j)"),
             )
 
-        quantize_x(0, 0, HALF_S)
+        first_scales = keep.tile([P, QUARTER_S], U8, name="first_scales", align_bytes=64)
+        x_scales.append(first_scales[:])
+        quantize_x(0)
         quantize_w(0)
-        x_codes.append(keep.tile([P, HALF_S], U32, name="x_codes1", tag="picked0", align_bytes=64))
-        x_scales.append(keep.tile([P, HALF_S], U8, name="x_scales1", tag="w_grouped0", align_bytes=64))
-        for c0, c1 in LATE_PIECES:
-            quantize_x(1, c0, c1)
+        late_scales = keep.tile([P, S - QUARTER_S], U8, name="late_scales", tag="w_grouped0", align_bytes=64)
+        for n in range(1, len(PIECES)):
+            x_scales.append(late_scales[:, PIECES[n][0] - QUARTER_S : PIECES[n][1] - QUARTER_S])
+            quantize_x(n)
+        group_w(1, 1, nc.vector.tensor_copy)
         quantize_w(1)
 
-        h_first = keep.tile([P, S], F32, name="h_first")
+        h_first = keep.tile([P, S], F32, name="h_first", tag="w_raw0")
         h_rest = keep.tile([P, PACK - 1, S], F32, name="h_rest")
         h = [h_first[:]] + [h_rest[:, t, :] for t in range(PACK - 1)]
 
-        def product(dst, t, s, c0, c1):
+        def product(dst, t, n):
+            c0, c1 = PIECES[n]
             nc.tensor.matmul_mx(
                 out=dst,
                 lhsT=w_codes[:, t * P : (t + 1) * P].bitcast(FP8X4),
                 lhsT_scale=w_scales[:, t * P : (t + 1) * P],
-                rhs=x_codes[s][:, c0:c1].bitcast(FP8X4),
-                rhs_scale=x_scales[s][:, c0:c1],
+                rhs=x_codes[:, c0:c1].bitcast(FP8X4),
+                rhs_scale=x_scales[n],
                 start=True,
                 stop=True,
             )
@@ -181,53 +184,57 @@ def tile_picked_pna_silu_e_kernel(
         def silu(dst, src):
             nc.scalar.activation(dst, src, ACT.Silu, bias=zero_bias[:])
 
-        acc = bank(4, [P, HALF_S])
-        product(acc[:], 0, 0, 0, HALF_S)
-        silu(h[0][:, 0:HALF_S], acc[:])
-        for n, (c0, c1) in enumerate(LATE_PIECES):
-            acc = bank(5 + n, [P, c1 - c0])
-            product(acc[:], 0, 1, c0, c1)
-            silu(h[0][:, HALF_S + c0 : HALF_S + c1], acc[:])
-        last0, last1 = LATE_PIECES[-1]
+        def h_stretch(bank_no, t, first, end):
+            c0, c1 = PIECES[first][0], PIECES[end - 1][1]
+            acc = bank(bank_no, [P, c1 - c0])
+            for n in range(first, end):
+                product(acc[:, PIECES[n][0] - c0 : PIECES[n][1] - c0], t, n)
+            silu(h[t][:, c0:c1], acc[:])
+
+        last = len(PIECES) - 1
+        for n, bank_no in enumerate((4, 5, 6, 7, 3)):
+            h_stretch(bank_no, 0, n, n + 1)
         for t in range(1, PACK):
-            acc = bank(4 + (2 * t) % 4, [P, HALF_S])
-            product(acc[:], t, 0, 0, HALF_S)
-            silu(h[t][:, 0:HALF_S], acc[:])
-            acc = bank(4 + (2 * t + 1) % 4, [P, last0])
-            for c0, c1 in LATE_PIECES[:-1]:
-                product(acc[:, c0:c1], t, 1, c0, c1)
-            silu(h[t][:, HALF_S : HALF_S + last0], acc[:])
+            h_stretch(4 + (2 * t) % 4, t, 0, 2)
+            h_stretch(4 + (2 * t + 1) % 4, t, 2, last)
+        last0, last1 = PIECES[last]
         acc = bank(4, [P, PACK - 1, last1 - last0])
         for t in range(1, PACK):
-            product(acc[:, t - 1, :], t, 1, last0, last1)
-        silu(h_rest[:, :, HALF_S + last0 : HALF_S + last1], acc[:])
+            product(acc[:, t - 1, :], t, last)
+        silu(h_rest[:, :, last0:last1], acc[:])
 
-        fetched = [keep.tile([P, PACK, V], F32, name="fetched%d" % d) for d in range(DEG)]
-        rounded = [keep.tile([P, V, PACK], BF16, name="rounded%d" % d) for d in range(DEG)]
+        lots = [(d, 0, V) for d in range(DEG - 1)] + [(DEG - 1, 0, HALF_V), (DEG - 1, HALF_V, V)]
+        fetched = [
+            keep.tile([P, PACK, v1 - v0], F32, name="fetched%d" % n, tag="w_grouped1" if n == 0 else "fetched%d" % n, align_bytes=64)
+            for n, (d, v0, v1) in enumerate(lots)
+        ]
+        rounded = [keep.tile([P, v1 - v0, PACK], BF16, name="rounded%d" % n) for n, (d, v0, v1) in enumerate(lots)]
 
-        def round_fetched(d, v0, v1):
+        def round_fetched(n):
             nc.scalar.copy(
-                out=rounded[d][:, v0:v1, :].rearrange("p (c i) t -> p c t i", i=4),
-                in_=fetched[d][:, :, v0:v1].rearrange("p t (c i) -> p c t i", i=4),
+                out=rounded[n][:].rearrange("p (c i) t -> p c t i", i=4),
+                in_=fetched[n][:].rearrange("p t (c i) -> p c t i", i=4),
             )
 
         sum_t = [bank(vb, [P, PACK, P]) for vb in range(V // P)]
-        order = [(0, d) for d in range(DEG)] + [(t, d) for d in range(DEG) for t in range(1, PACK)]
-        for n, (t, d) in enumerate(order):
-            nc.vector.tensor_copy(out=fetched[d][:, t, :], in_=h[t].indirect(pos_sb[d][:]))
-            for vb in range(V // P):
+        order = [(0, n) for n in range(len(lots))] + [(t, n) for n in range(len(lots)) for t in range(1, PACK)]
+        for t, n in order:
+            d, v0, v1 = lots[n]
+            offsets = pos_sb[d][:, v0 // PER_COLUMN : v1 // PER_COLUMN]
+            nc.vector.tensor_copy(out=fetched[n][:, t, :], in_=h[t].indirect(offsets))
+            for vb in range(v0 // P, v1 // P):
                 nc.tensor.matmul(
                     sum_t[vb][:, t, :],
-                    lhsT=fetched[d][:, t, vb * P : (vb + 1) * P],
+                    lhsT=fetched[n][:, t, vb * P - v0 : (vb + 1) * P - v0],
                     rhs=ident[:],
                     is_transpose=True,
-                    start=(n == 0),
-                    stop=(n == len(order) - 1),
+                    start=(t == 0 and d == 0),
+                    stop=(t == PACK - 1 and d == DEG - 1),
                 )
             if t == PACK - 1 and d < DEG - 1:
-                round_fetched(d, 0, V)
+                round_fetched(n)
 
-        flat = [rounded[d][:].rearrange("p v t -> p (v t)") for d in range(DEG)]
+        flat = [r[:].rearrange("p v t -> p (v t)") for r in rounded]
         hi_run, lo_run = flat[0], flat[0]
         for d in range(1, DEG - 1):
             hi_next = keep.tile([P, V * PACK], BF16, name="hi%d" % d)
@@ -238,8 +245,6 @@ def tile_picked_pna_silu_e_kernel(
 
         blocks = HALF_V // P
         for half in range(2):
-            round_fetched(DEG - 1, half * HALF_V, (half + 1) * HALF_V)
-
             back = bank(4 + half, [P, 2, HALF_V])
             for r in range(blocks):
                 vb = half * blocks + r
@@ -250,47 +255,47 @@ def tile_picked_pna_silu_e_kernel(
                 mean_words = mean_t[:].rearrange("v u p e -> v (u p e)").bitcast(F32)
                 for u in range(2):
                     nc.tensor.transpose(back[:, u, r * P : (r + 1) * P], mean_words[:, u * P : (u + 1) * P], ident[:])
-            mean = []
-            for r in range(blocks):
-                mean_name = "mean%d_%d" % (half, r)
-                mean_block = keep.tile([P, P * PACK], BF16, name=mean_name, tag=mean_name, align_bytes=64)
-                nc.scalar.copy(
-                    out=mean_block[:].bitcast(F32).rearrange("p (v u) -> p v u", u=2),
-                    in_=back[:, :, r * P : (r + 1) * P].rearrange("p u v -> p v u"),
-                )
-                mean.append(mean_block[:])
+            round_fetched(DEG - 1 + half)
+            mean = keep.tile([P, HALF_V * PACK], BF16, name="mean%d" % half, tag="mean%d" % half, align_bytes=64)
+            nc.scalar.copy(
+                out=mean[:].bitcast(F32).rearrange("p (v u) -> p v u", u=2),
+                in_=back[:].rearrange("p u v -> p v u"),
+            )
 
             cols = slice(half * HALF_V * PACK, (half + 1) * HALF_V * PACK)
             extremes = keep.tile(
-                [P, 2, HALF_V * PACK], BF16, name="extremes%d" % half, tag=("extremes0", "mean0_0")[half], align_bytes=64
+                [P, 2, HALF_V * PACK], BF16, name="extremes%d" % half, tag=("extremes0", "mean0")[half], align_bytes=64
             )
             hi, lo = extremes[:, 0, :], extremes[:, 1, :]
-            nc.vector.tensor_tensor(out=hi, in0=hi_run[:, cols], in1=flat[DEG - 1][:, cols], op=ALU.max)
-            nc.vector.tensor_tensor(out=lo, in0=lo_run[:, cols], in1=flat[DEG - 1][:, cols], op=ALU.min)
+            nc.vector.tensor_tensor(out=hi, in0=hi_run[:, cols], in1=flat[DEG - 1 + half], op=ALU.max)
+            nc.vector.tensor_tensor(out=lo, in0=lo_run[:, cols], in1=flat[DEG - 1 + half], op=ALU.min)
 
-            z_codes, z_scales = {}, {}
-            for a, pieces in ((LARGEST, [hi]), (SMALLEST, [lo]), (MEAN, mean)):
-                width = HALF_V // len(pieces)
-                z_codes[a] = keep.tile([P, HALF_V], U32, name="z_codes%d_%d" % (a, half), align_bytes=64)
-                z_scales[a] = keep.tile([P, HALF_V], U8, name="z_scales%d_%d" % (a, half), align_bytes=64)
-                for n, z in enumerate(pieces):
-                    nc.vector.quantize_mx(
-                        out=z_codes[a][:, n * width : (n + 1) * width].bitcast(FP8X4),
-                        scales=z_scales[a][:, n * width : (n + 1) * width],
-                        in_=z,
-                    )
+            z_codes = keep.tile([P, 3 * HALF_V], U32, name="z_codes%d" % half, align_bytes=64)
+            z_scales = keep.tile([P, 3 * HALF_V], U8, name="z_scales%d" % half, align_bytes=64)
+
+            def quantize_z(c0, z):
+                c1 = c0 + z.shape[1] // PACK
+                nc.vector.quantize_mx(out=z_codes[:, c0:c1].bitcast(FP8X4), scales=z_scales[:, c0:c1], in_=z)
+
+            quantize_z(MEAN * HALF_V, mean[:])
+            if half == 0:
+                quantize_z(LARGEST * HALF_V, extremes[:].rearrange("p a c -> p (a c)"))
+            else:
+                quantize_z(LARGEST * HALF_V, hi)
+                for r in range(blocks):
+                    quantize_z(SMALLEST * HALF_V + r * P, lo[:, r * P * PACK : (r + 1) * P * PACK])
 
             res_banks = ((0, 1, 6, 7), (2, 3, 4, 6))[half]
             res = [bank(n, [P, P]) for n in res_banks]
-            for n, a in enumerate((LARGEST, SMALLEST, MEAN)):
+            for n, a in enumerate((MEAN, LARGEST, SMALLEST)):
                 for r in range(blocks):
                     for m in range(N // P):
                         nc.tensor.matmul_mx(
                             out=res[blocks * m + r][:],
                             lhsT=wq_words[a][:, m * 2 * P : (m + 1) * 2 * P].bitcast(FP4X4),
                             lhsT_scale=wq_scales[:, a * N + m * P : a * N + (m + 1) * P],
-                            rhs=z_codes[a][:, r * P : (r + 1) * P].bitcast(FP8X4),
-                            rhs_scale=z_scales[a][:, r * P : (r + 1) * P],
+                            rhs=z_codes[:, a * HALF_V + r * P : a * HALF_V + (r + 1) * P].bitcast(FP8X4),
+                            rhs_scale=z_scales[:, a * HALF_V + r * P : a * HALF_V + (r + 1) * P],
                             start=(n == 0),
                             stop=(n == 2),
                         )

@@ -26,9 +26,7 @@ QUARTER_S = S // 4
 HALF_V = V // 2
 MEAN, LARGEST, SMALLEST = 0, 1, 2
 
-X_LOADS = ((0, 0, 1280, 0), (0, 1280, 2048, 384), (1, 0, 1024, 640), (1, 1024, 1792, 256), (1, 1792, 2048, 64))
 PIECES = ((0, 256), (256, 512), (512, 768), (768, 896), (896, 1024))
-W_LOADS = 2
 
 
 def tile_picked_pna_silu_e_kernel(
@@ -52,22 +50,17 @@ def tile_picked_pna_silu_e_kernel(
         wq_scales = keep.tile([P, 3 * N], U8, name="wq_scales", align_bytes=64)
         nc.gpsimd.memset(wq_scales[:], 0)
 
-        x_rows = xT.rearrange("(p u e) t -> p u e t", u=2, e=2)
-        x_raw = []
+        x_rows = xT.rearrange("(p j) t -> p j t", j=PACK)
+        x_plane = []
         offs_sb = lists.tile([P, S // PER_COLUMN], U16, name="offs_sb")
-        for n, (u, c0, c1, share) in enumerate(X_LOADS):
-            raw = keep.tile([P, 2, c1 - c0], F32, name="x_raw%d" % n)
-            nc.sync.dma_start(out=raw[:], in_=x_rows[:, u, :, c0:c1])
-            x_raw.append(raw)
-            if n == 0:
+        for j in range(PACK):
+            plane = keep.tile([P, T], F32, name="x_plane%d" % j)
+            nc.sync.dma_start(out=plane[:], in_=x_rows[:, j, :])
+            x_plane.append(plane)
+            if j == 0:
                 nc.sync.dma_start(offs_sb[:], offs)
-        w_rows = w1.rearrange("(p j) c -> p j c", j=PACK)
-        w_width = H // W_LOADS
-        w_raw = []
-        for n in range(W_LOADS):
-            raw = keep.tile([P, PACK, w_width], F32, name="w_raw%d" % n, tag="w_raw%d" % n)
-            nc.sync.dma_start(out=raw[:], in_=w_rows[:, :, n * w_width : (n + 1) * w_width])
-            w_raw.append(raw)
+        w_raw = keep.tile([P, PACK, H], F32, name="w_raw")
+        nc.sync.dma_start(out=w_raw[:], in_=w1.rearrange("(p j) c -> p j c", j=PACK))
         pos_sb = []
         for d, pos in enumerate((pos1, pos2, pos3, pos4)):
             pos_tile = lists.tile([P, V // PER_COLUMN], U16, name="pos_sb%d" % d)
@@ -85,52 +78,47 @@ def tile_picked_pna_silu_e_kernel(
                     in_=scales_hbm[0, 4 * q : 4 * q + 4, :].bitcast(I32),
                 )
 
-        pairs = [keep.tile([P, T, 2], BF16, name="pairs%d" % u) for u in range(2)]
-        picked_pair = keep.tile([P, 2, S], I32, name="picked_pair")
-        woven = [keep.tile([P, QUARTER_S, 2], I32, name="woven%d" % q, align_bytes=64) for q in range(4)]
+        picked = [keep.tile([P, 2, S], BF16, name="picked%d" % u) for u in range(2)]
+        woven = [
+            keep.tile([P, QUARTER_S, PACK], BF16, name="woven%d" % q, tag="woven%d" % q, align_bytes=64) for q in range(4)
+        ]
 
-        def round_x(n):
-            u, c0, c1, share = X_LOADS[n]
-            for a, b, copy in ((0, share, nc.scalar.copy), (share, c1 - c0, nc.vector.tensor_copy)):
-                if b > a:
-                    copy(
-                        out=pairs[u][:, c0 + a : c0 + b, :].rearrange("p (c i) e -> p c e i", i=4),
-                        in_=x_raw[n][:, :, a:b].rearrange("p e (c i) -> p c e i", i=4),
-                    )
-
-        def gather_x(dst, u, c0, c1):
-            window = pairs[u][:].rearrange("p t e -> p (t e)").bitcast(U32)
+        def gather_x(j, c0, c1):
             offsets = offs_sb[:, c0 // PER_COLUMN : c1 // PER_COLUMN]
-            nc.vector.tensor_copy(out=dst.bitcast(U32), in_=window.indirect(offsets))
+            nc.vector.tensor_copy(out=picked[j // 2][:, j % 2, c0:c1], in_=x_plane[j][:].indirect(offsets))
 
-        round_x(0)
-        round_x(1)
-        gather_x(picked_pair[:, 0, :], 0, 0, S)
-        for n in range(2, len(X_LOADS)):
-            round_x(n)
-        for q in range(4):
-            cols = slice(q * QUARTER_S, (q + 1) * QUARTER_S)
-            gather_x(picked_pair[:, 1, cols], 1, cols.start, cols.stop)
+        def weave(u, q):
             nc.scalar.copy(
-                out=woven[q][:].rearrange("p (c i) u -> p c u i", i=2).bitcast(U32),
-                in_=picked_pair[:, :, cols].rearrange("p u (c i) -> p c u i", i=2).bitcast(U32),
+                out=woven[q][:, :, 2 * u : 2 * u + 2],
+                in_=picked[u][:, :, q * QUARTER_S : (q + 1) * QUARTER_S].rearrange("p e c -> p c e"),
             )
+
+        plane0_rounded = keep.tile([P, T], BF16, name="plane0_rounded")
+        nc.scalar.copy(out=plane0_rounded[:], in_=x_plane[0][:])
+        cut = S - QUARTER_S
+        nc.scalar.activation(picked[0][:, 0, cut:S], plane0_rounded[:].indirect(offs_sb[:, cut // PER_COLUMN :]), ACT.Copy)
+        gather_x(0, 0, cut)
+        for c0 in range(0, S, HALF_S):
+            gather_x(1, c0, c0 + HALF_S)
+            for q in range(c0 // QUARTER_S, (c0 + HALF_S) // QUARTER_S):
+                weave(0, q)
+        gather_x(2, 0, S)
+        for q in range(4):
+            gather_x(3, q * QUARTER_S, (q + 1) * QUARTER_S)
+            weave(1, q)
 
         w_grouped = [
             keep.tile([P, 2, P, PACK], BF16, name="w_grouped%d" % g, tag="w_grouped%d" % g, align_bytes=64)
             for g in range(2)
         ]
 
-        def group_w(g, n, copy):
-            m_width = P // W_LOADS
-            copy(
-                out=w_grouped[g][:, :, n * m_width : (n + 1) * m_width, :].rearrange("p e m j -> p m j e"),
-                in_=w_raw[n][:].rearrange("p j (m t) -> p m j t", t=PACK)[:, :, :, 2 * g : 2 * g + 2],
+        def group_w(g, m0, m1):
+            nc.vector.tensor_copy(
+                out=w_grouped[g][:, :, m0:m1, :].rearrange("p e m j -> p m j e"),
+                in_=w_raw[:].rearrange("p j (m t) -> p m j t", t=PACK)[:, m0:m1, :, 2 * g : 2 * g + 2],
             )
 
-        group_w(0, 0, nc.vector.tensor_copy)
-        group_w(0, 1, nc.vector.tensor_copy)
-        group_w(1, 0, nc.scalar.copy)
+        group_w(0, 0, P)
 
         x_codes = keep.tile([P, S], U32, name="x_codes", align_bytes=64)
         w_codes = keep.tile([P, H], U32, name="w_codes", align_bytes=64)
@@ -144,7 +132,7 @@ def tile_picked_pna_silu_e_kernel(
             nc.vector.quantize_mx(
                 out=x_codes[:, c0:c1].bitcast(FP8X4),
                 scales=x_scales[n],
-                in_=src.rearrange("p s u -> p (s u)").bitcast(BF16),
+                in_=src.rearrange("p s j -> p (s j)"),
             )
 
         def quantize_w(g):
@@ -158,14 +146,15 @@ def tile_picked_pna_silu_e_kernel(
         x_scales.append(first_scales[:])
         quantize_x(0)
         quantize_w(0)
+        group_w(1, 0, P // 2)
+        group_w(1, P // 2, P)
         late_scales = keep.tile([P, S - QUARTER_S], U8, name="late_scales", tag="w_grouped0", align_bytes=64)
         for n in range(1, len(PIECES)):
             x_scales.append(late_scales[:, PIECES[n][0] - QUARTER_S : PIECES[n][1] - QUARTER_S])
             quantize_x(n)
-        group_w(1, 1, nc.vector.tensor_copy)
         quantize_w(1)
 
-        h_first = keep.tile([P, S], F32, name="h_first", tag="w_raw0")
+        h_first = keep.tile([P, S], F32, name="h_first")
         h_rest = keep.tile([P, PACK - 1, S], F32, name="h_rest")
         h = [h_first[:]] + [h_rest[:, t, :] for t in range(PACK - 1)]
 
@@ -194,18 +183,18 @@ def tile_picked_pna_silu_e_kernel(
         last = len(PIECES) - 1
         for n, bank_no in enumerate((4, 5, 6, 7, 3)):
             h_stretch(bank_no, 0, n, n + 1)
-        for t in range(1, PACK):
-            h_stretch(4 + (2 * t) % 4, t, 0, 2)
-            h_stretch(4 + (2 * t + 1) % 4, t, 2, last)
+        for t, banks in ((1, (6, 7)), (2, (0, 1)), (3, (2, 4))):
+            h_stretch(banks[0], t, 0, 2)
+            h_stretch(banks[1], t, 2, last)
         last0, last1 = PIECES[last]
-        acc = bank(4, [P, PACK - 1, last1 - last0])
+        acc = bank(5, [P, PACK - 1, last1 - last0])
         for t in range(1, PACK):
             product(acc[:, t - 1, :], t, last)
         silu(h_rest[:, :, last0:last1], acc[:])
 
         lots = [(d, 0, V) for d in range(DEG - 1)] + [(DEG - 1, 0, HALF_V), (DEG - 1, HALF_V, V)]
         fetched = [
-            keep.tile([P, PACK, v1 - v0], F32, name="fetched%d" % n, tag="w_grouped1" if n == 0 else "fetched%d" % n, align_bytes=64)
+            keep.tile([P, PACK, v1 - v0], F32, name="fetched%d" % n)
             for n, (d, v0, v1) in enumerate(lots)
         ]
         rounded = [keep.tile([P, v1 - v0, PACK], BF16, name="rounded%d" % n) for n, (d, v0, v1) in enumerate(lots)]
@@ -244,11 +233,12 @@ def tile_picked_pna_silu_e_kernel(
             hi_run, lo_run = hi_next[:], lo_next[:]
 
         blocks = HALF_V // P
+        means = []
         for half in range(2):
             back = bank(4 + half, [P, 2, HALF_V])
             for r in range(blocks):
                 vb = half * blocks + r
-                mean_t = keep.tile([P, 2, P, 2], BF16, name="mean_t%d" % vb)
+                mean_t = keep.tile([P, 2, P, 2], BF16, name="mean_t%d" % vb, tag="mean_t%d" % vb)
                 nc.scalar.activation(
                     mean_t[:], sum_t[vb][:].rearrange("v (u e) p -> v u p e", e=2), ACT.Copy, scale=1.0 / DEG
                 )
@@ -261,6 +251,10 @@ def tile_picked_pna_silu_e_kernel(
                 out=mean[:].bitcast(F32).rearrange("p (v u) -> p v u", u=2),
                 in_=back[:].rearrange("p u v -> p v u"),
             )
+            means.append(mean)
+
+        for half in range(2):
+            mean = means[half]
 
             cols = slice(half * HALF_V * PACK, (half + 1) * HALF_V * PACK)
             extremes = keep.tile(
@@ -285,7 +279,7 @@ def tile_picked_pna_silu_e_kernel(
                 for r in range(blocks):
                     quantize_z(SMALLEST * HALF_V + r * P, lo[:, r * P * PACK : (r + 1) * P * PACK])
 
-            res_banks = ((0, 1, 6, 7), (2, 3, 4, 6))[half]
+            res_banks = ((0, 1, 6, 7), (2, 3, 4, 5))[half]
             res = [bank(n, [P, P]) for n in res_banks]
             for n, a in enumerate((MEAN, LARGEST, SMALLEST)):
                 for r in range(blocks):
@@ -299,7 +293,10 @@ def tile_picked_pna_silu_e_kernel(
                             start=(n == 0),
                             stop=(n == 2),
                         )
-            staged = [keep.tile([P, HALF_V], F32, name="staged%d_%d" % (m, half)) for m in range(N // P)]
+            staged = [
+                keep.tile([P, HALF_V], F32, name="staged%d_%d" % (m, half), tag="mean_t%d" % (2 * (1 - half) + m))
+                for m in range(N // P)
+            ]
             for r in range(blocks):
                 for m in range(N // P):
                     very_last = half == 1 and r == blocks - 1 and m == N // P - 1

@@ -24,6 +24,7 @@ PER_COLUMN = 16
 HALF_S = S // 2
 QUARTER_S = S // 4
 HALF_V = V // 2
+BLOCKS = HALF_V // P
 MEAN, LARGEST, SMALLEST = 0, 1, 2
 
 PIECES = ((0, 256), (256, 512), (512, 768), (768, 896), (896, 1024))
@@ -40,6 +41,9 @@ def tile_picked_pna_silu_e_kernel(
 
         def bank(n, shape):
             return psum.tile(shape, F32, name="bank%d" % n, tag="bank%d" % n)
+
+        def entries(list_tile, c0, c1):
+            return list_tile[:, c0 // PER_COLUMN : c1 // PER_COLUMN]
 
         zero_in = keep.tile([P, 1], F32, name="zero_in")
         zero_bias = keep.tile([P, 1], F32, name="zero_bias")
@@ -79,13 +83,10 @@ def tile_picked_pna_silu_e_kernel(
                 )
 
         picked = [keep.tile([P, 2, S], BF16, name="picked%d" % u) for u in range(2)]
-        woven = [
-            keep.tile([P, QUARTER_S, PACK], BF16, name="woven%d" % q, tag="woven%d" % q, align_bytes=64) for q in range(4)
-        ]
+        woven = [keep.tile([P, QUARTER_S, PACK], BF16, name="woven%d" % q, align_bytes=64) for q in range(4)]
 
         def gather_x(j, c0, c1):
-            offsets = offs_sb[:, c0 // PER_COLUMN : c1 // PER_COLUMN]
-            nc.vector.tensor_copy(out=picked[j // 2][:, j % 2, c0:c1], in_=x_plane[j][:].indirect(offsets))
+            nc.vector.tensor_copy(out=picked[j // 2][:, j % 2, c0:c1], in_=x_plane[j][:].indirect(entries(offs_sb, c0, c1)))
 
         def weave(u, q):
             nc.scalar.copy(
@@ -95,9 +96,10 @@ def tile_picked_pna_silu_e_kernel(
 
         plane0_rounded = keep.tile([P, T], BF16, name="plane0_rounded")
         nc.scalar.copy(out=plane0_rounded[:], in_=x_plane[0][:])
-        cut = S - QUARTER_S
-        nc.scalar.activation(picked[0][:, 0, cut:S], plane0_rounded[:].indirect(offs_sb[:, cut // PER_COLUMN :]), ACT.Copy)
-        gather_x(0, 0, cut)
+        nc.scalar.activation(
+            picked[0][:, 0, S - QUARTER_S : S], plane0_rounded[:].indirect(entries(offs_sb, S - QUARTER_S, S)), ACT.Copy
+        )
+        gather_x(0, 0, S - QUARTER_S)
         for c0 in range(0, S, HALF_S):
             gather_x(1, c0, c0 + HALF_S)
             for q in range(c0 // QUARTER_S, (c0 + HALF_S) // QUARTER_S):
@@ -111,28 +113,15 @@ def tile_picked_pna_silu_e_kernel(
             keep.tile([P, 2, P, PACK], BF16, name="w_grouped%d" % g, tag="w_grouped%d" % g, align_bytes=64)
             for g in range(2)
         ]
-
-        def group_w(g, m0, m1):
-            nc.vector.tensor_copy(
-                out=w_grouped[g][:, :, m0:m1, :].rearrange("p e m j -> p m j e"),
-                in_=w_raw[:].rearrange("p j (m t) -> p m j t", t=PACK)[:, m0:m1, :, 2 * g : 2 * g + 2],
-            )
-
-        group_w(0, 0, P)
-
         x_codes = keep.tile([P, S], U32, name="x_codes", align_bytes=64)
         w_codes = keep.tile([P, H], U32, name="w_codes", align_bytes=64)
         w_scales = keep.tile([P, H], U8, name="w_scales", align_bytes=64)
         x_scales = []
 
-        def quantize_x(n):
-            c0, c1 = PIECES[n]
-            q = c0 // QUARTER_S
-            src = woven[q][:, c0 - q * QUARTER_S : c1 - q * QUARTER_S, :]
-            nc.vector.quantize_mx(
-                out=x_codes[:, c0:c1].bitcast(FP8X4),
-                scales=x_scales[n],
-                in_=src.rearrange("p s j -> p (s j)"),
+        def group_w(g, m0, m1):
+            nc.vector.tensor_copy(
+                out=w_grouped[g][:, :, m0:m1, :].rearrange("p e m j -> p m j e"),
+                in_=w_raw[:].rearrange("p j (m t) -> p m j t", t=PACK)[:, m0:m1, :, 2 * g : 2 * g + 2],
             )
 
         def quantize_w(g):
@@ -142,6 +131,16 @@ def tile_picked_pna_silu_e_kernel(
                 in_=w_grouped[g][:].rearrange("p e m j -> p (e m j)"),
             )
 
+        def quantize_x(n):
+            c0, c1 = PIECES[n]
+            q = c0 // QUARTER_S
+            nc.vector.quantize_mx(
+                out=x_codes[:, c0:c1].bitcast(FP8X4),
+                scales=x_scales[n],
+                in_=woven[q][:, c0 - q * QUARTER_S : c1 - q * QUARTER_S, :].rearrange("p s j -> p (s j)"),
+            )
+
+        group_w(0, 0, P)
         first_scales = keep.tile([P, QUARTER_S], U8, name="first_scales", align_bytes=64)
         x_scales.append(first_scales[:])
         quantize_x(0)
@@ -154,9 +153,9 @@ def tile_picked_pna_silu_e_kernel(
             quantize_x(n)
         quantize_w(1)
 
-        h_first = keep.tile([P, S], F32, name="h_first")
-        h_rest = keep.tile([P, PACK - 1, S], F32, name="h_rest")
-        h = [h_first[:]] + [h_rest[:, t, :] for t in range(PACK - 1)]
+        h_early = [keep.tile([P, S], F32, name="h%d" % t) for t in range(2)]
+        h_late = keep.tile([P, 2, S], F32, name="h_late")
+        h = [h_early[0][:], h_early[1][:], h_late[:, 0, :], h_late[:, 1, :]]
 
         def product(dst, t, n):
             c0, c1 = PIECES[n]
@@ -183,45 +182,39 @@ def tile_picked_pna_silu_e_kernel(
         last = len(PIECES) - 1
         for n, bank_no in enumerate((4, 5, 6, 7, 3)):
             h_stretch(bank_no, 0, n, n + 1)
-        for t, banks in ((1, (6, 7)), (2, (0, 1)), (3, (2, 4))):
+        h_stretch(6, 1, 0, 2)
+        h_stretch(7, 1, 2, last + 1)
+        for t, banks in ((2, (0, 1)), (3, (2, 4))):
             h_stretch(banks[0], t, 0, 2)
             h_stretch(banks[1], t, 2, last)
         last0, last1 = PIECES[last]
-        acc = bank(5, [P, PACK - 1, last1 - last0])
-        for t in range(1, PACK):
-            product(acc[:, t - 1, :], t, last)
-        silu(h_rest[:, :, last0:last1], acc[:])
+        acc = bank(5, [P, 2, last1 - last0])
+        for e in range(2):
+            product(acc[:, e, :], 2 + e, last)
+        silu(h_late[:, :, last0:last1], acc[:])
 
-        lots = [(d, 0, V) for d in range(DEG - 1)] + [(DEG - 1, 0, HALF_V), (DEG - 1, HALF_V, V)]
-        fetched = [
-            keep.tile([P, PACK, v1 - v0], F32, name="fetched%d" % n)
-            for n, (d, v0, v1) in enumerate(lots)
-        ]
-        rounded = [keep.tile([P, v1 - v0, PACK], BF16, name="rounded%d" % n) for n, (d, v0, v1) in enumerate(lots)]
+        fetched = [[keep.tile([P, 2, V], F32, name="fetched%d_%d" % (d, u)) for u in range(2)] for d in range(DEG)]
+        rounded = [keep.tile([P, V, PACK], BF16, name="rounded%d" % d) for d in range(DEG)]
 
-        def round_fetched(n):
-            nc.scalar.copy(
-                out=rounded[n][:].rearrange("p (c i) t -> p c t i", i=4),
-                in_=fetched[n][:].rearrange("p t (c i) -> p c t i", i=4),
-            )
+        def round_fetched(d, u):
+            nc.scalar.copy(out=rounded[d][:, :, 2 * u : 2 * u + 2], in_=fetched[d][u][:].rearrange("p e v -> p v e"))
 
-        sum_t = [bank(vb, [P, PACK, P]) for vb in range(V // P)]
-        order = [(0, n) for n in range(len(lots))] + [(t, n) for n in range(len(lots)) for t in range(1, PACK)]
-        for t, n in order:
-            d, v0, v1 = lots[n]
-            offsets = pos_sb[d][:, v0 // PER_COLUMN : v1 // PER_COLUMN]
-            nc.vector.tensor_copy(out=fetched[n][:, t, :], in_=h[t].indirect(offsets))
-            for vb in range(v0 // P, v1 // P):
+        sum_t = [bank(b, [P, PACK, P]) for b in range(V // P)]
+        order = [(t, d) for t in range(2) for d in range(DEG)] + [(t, d) for d in range(DEG) for t in range(2, PACK)]
+        for n, (t, d) in enumerate(order):
+            dst = fetched[d][t // 2][:, t % 2, :]
+            nc.vector.tensor_copy(out=dst, in_=h[t].indirect(pos_sb[d][:]))
+            for b in range(V // P):
                 nc.tensor.matmul(
-                    sum_t[vb][:, t, :],
-                    lhsT=fetched[n][:, t, vb * P - v0 : (vb + 1) * P - v0],
+                    sum_t[b][:, t, :],
+                    lhsT=dst[:, b * P : (b + 1) * P],
                     rhs=ident[:],
                     is_transpose=True,
-                    start=(t == 0 and d == 0),
-                    stop=(t == PACK - 1 and d == DEG - 1),
+                    start=(n == 0),
+                    stop=(n == len(order) - 1),
                 )
-            if t == PACK - 1 and d < DEG - 1:
-                round_fetched(n)
+            if t % 2 == 1 and n < len(order) - 1:
+                round_fetched(d, t // 2)
 
         flat = [r[:].rearrange("p v t -> p (v t)") for r in rounded]
         hi_run, lo_run = flat[0], flat[0]
@@ -232,20 +225,20 @@ def tile_picked_pna_silu_e_kernel(
             nc.vector.tensor_tensor(out=lo_next[:], in0=lo_run, in1=flat[d], op=ALU.min)
             hi_run, lo_run = hi_next[:], lo_next[:]
 
-        blocks = HALF_V // P
         means = []
         for half in range(2):
             back = bank(4 + half, [P, 2, HALF_V])
-            for r in range(blocks):
-                vb = half * blocks + r
-                mean_t = keep.tile([P, 2, P, 2], BF16, name="mean_t%d" % vb, tag="mean_t%d" % vb)
+            for r in range(BLOCKS):
+                b = half * BLOCKS + r
+                mean_t = keep.tile([P, 2, P, 2], BF16, name="mean_t%d" % b, tag="mean_t%d" % b)
                 nc.scalar.activation(
-                    mean_t[:], sum_t[vb][:].rearrange("v (u e) p -> v u p e", e=2), ACT.Copy, scale=1.0 / DEG
+                    mean_t[:], sum_t[b][:].rearrange("v (u e) p -> v u p e", e=2), ACT.Copy, scale=1.0 / DEG
                 )
                 mean_words = mean_t[:].rearrange("v u p e -> v (u p e)").bitcast(F32)
                 for u in range(2):
                     nc.tensor.transpose(back[:, u, r * P : (r + 1) * P], mean_words[:, u * P : (u + 1) * P], ident[:])
-            round_fetched(DEG - 1 + half)
+            if half == 0:
+                round_fetched(DEG - 1, 1)
             mean = keep.tile([P, HALF_V * PACK], BF16, name="mean%d" % half, tag="mean%d" % half, align_bytes=64)
             nc.scalar.copy(
                 out=mean[:].bitcast(F32).rearrange("p (v u) -> p v u", u=2),
@@ -254,15 +247,13 @@ def tile_picked_pna_silu_e_kernel(
             means.append(mean)
 
         for half in range(2):
-            mean = means[half]
-
             cols = slice(half * HALF_V * PACK, (half + 1) * HALF_V * PACK)
             extremes = keep.tile(
                 [P, 2, HALF_V * PACK], BF16, name="extremes%d" % half, tag=("extremes0", "mean0")[half], align_bytes=64
             )
             hi, lo = extremes[:, 0, :], extremes[:, 1, :]
-            nc.vector.tensor_tensor(out=hi, in0=hi_run[:, cols], in1=flat[DEG - 1 + half], op=ALU.max)
-            nc.vector.tensor_tensor(out=lo, in0=lo_run[:, cols], in1=flat[DEG - 1 + half], op=ALU.min)
+            nc.vector.tensor_tensor(out=hi, in0=hi_run[:, cols], in1=flat[DEG - 1][:, cols], op=ALU.max)
+            nc.vector.tensor_tensor(out=lo, in0=lo_run[:, cols], in1=flat[DEG - 1][:, cols], op=ALU.min)
 
             z_codes = keep.tile([P, 3 * HALF_V], U32, name="z_codes%d" % half, align_bytes=64)
             z_scales = keep.tile([P, 3 * HALF_V], U8, name="z_scales%d" % half, align_bytes=64)
@@ -271,37 +262,43 @@ def tile_picked_pna_silu_e_kernel(
                 c1 = c0 + z.shape[1] // PACK
                 nc.vector.quantize_mx(out=z_codes[:, c0:c1].bitcast(FP8X4), scales=z_scales[:, c0:c1], in_=z)
 
-            quantize_z(MEAN * HALF_V, mean[:])
+            quantize_z(MEAN * HALF_V, means[half][:])
             if half == 0:
                 quantize_z(LARGEST * HALF_V, extremes[:].rearrange("p a c -> p (a c)"))
             else:
                 quantize_z(LARGEST * HALF_V, hi)
-                for r in range(blocks):
+                for r in range(BLOCKS):
                     quantize_z(SMALLEST * HALF_V + r * P, lo[:, r * P * PACK : (r + 1) * P * PACK])
 
-            res_banks = ((0, 1, 6, 7), (2, 3, 4, 5))[half]
-            res = [bank(n, [P, P]) for n in res_banks]
-            for n, a in enumerate((MEAN, LARGEST, SMALLEST)):
-                for r in range(blocks):
+            res = [bank(n, [P, P]) for n in ((0, 1, 6, 7), (2, 3, 4, 5))[half]]
+            for a in (MEAN, LARGEST, SMALLEST):
+                for r in range(BLOCKS):
+                    z_cols = slice(a * HALF_V + r * P, a * HALF_V + (r + 1) * P)
                     for m in range(N // P):
                         nc.tensor.matmul_mx(
-                            out=res[blocks * m + r][:],
+                            out=res[BLOCKS * m + r][:],
                             lhsT=wq_words[a][:, m * 2 * P : (m + 1) * 2 * P].bitcast(FP4X4),
                             lhsT_scale=wq_scales[:, a * N + m * P : a * N + (m + 1) * P],
-                            rhs=z_codes[:, a * HALF_V + r * P : a * HALF_V + (r + 1) * P].bitcast(FP8X4),
-                            rhs_scale=z_scales[:, a * HALF_V + r * P : a * HALF_V + (r + 1) * P],
-                            start=(n == 0),
-                            stop=(n == 2),
+                            rhs=z_codes[:, z_cols].bitcast(FP8X4),
+                            rhs_scale=z_scales[:, z_cols],
+                            start=(a == MEAN),
+                            stop=(a == SMALLEST),
                         )
+
             staged = [
-                keep.tile([P, HALF_V], F32, name="staged%d_%d" % (m, half), tag="mean_t%d" % (2 * (1 - half) + m))
+                keep.tile([P, HALF_V], F32, name="staged%d_%d" % (m, half), tag="mean_t%d" % (BLOCKS * (1 - half) + m))
                 for m in range(N // P)
             ]
-            for r in range(blocks):
+            if half == 0:
                 for m in range(N // P):
-                    very_last = half == 1 and r == blocks - 1 and m == N // P - 1
-                    copy = nc.vector.tensor_copy if very_last else nc.scalar.copy
-                    copy(out=staged[m][:, r * P : (r + 1) * P], in_=res[blocks * m + r][:])
-            for m in range(N // P):
-                queue = nc.scalar if (half == 1 and m == 0) else nc.sync
-                queue.dma_start(out=out[m * P : (m + 1) * P, half * HALF_V : (half + 1) * HALF_V], in_=staged[m][:])
+                    for r in range(BLOCKS):
+                        nc.scalar.copy(out=staged[m][:, r * P : (r + 1) * P], in_=res[BLOCKS * m + r][:])
+                    nc.sync.dma_start(out=out[m * P : (m + 1) * P, 0:HALF_V], in_=staged[m][:])
+            else:
+                for r in range(BLOCKS):
+                    for m in range(N // P):
+                        copy, queue = (nc.scalar.copy, nc.scalar) if m == r else (nc.vector.tensor_copy, nc.sync)
+                        block = staged[m][:, r * P : (r + 1) * P]
+                        copy(out=block, in_=res[BLOCKS * m + r][:])
+                        v0 = HALF_V + r * P
+                        queue.dma_start(out=out[m * P : (m + 1) * P, v0 : v0 + P], in_=block)

@@ -213,7 +213,7 @@ def tile_picked_pna_silu_e_kernel(
                     start=(n == 0),
                     stop=(n == len(order) - 1),
                 )
-            if t % 2 == 1 and n < len(order) - 1:
+            if t % 2 == 1:
                 round_fetched(d, t // 2)
 
         flat = [r[:].rearrange("p v t -> p (v t)") for r in rounded]
@@ -237,8 +237,6 @@ def tile_picked_pna_silu_e_kernel(
                 mean_words = mean_t[:].rearrange("v u p e -> v (u p e)").bitcast(F32)
                 for u in range(2):
                     nc.tensor.transpose(back[:, u, r * P : (r + 1) * P], mean_words[:, u * P : (u + 1) * P], ident[:])
-            if half == 0:
-                round_fetched(DEG - 1, 1)
             mean = keep.tile([P, HALF_V * PACK], BF16, name="mean%d" % half, tag="mean%d" % half, align_bytes=64)
             nc.scalar.copy(
                 out=mean[:].bitcast(F32).rearrange("p (v u) -> p v u", u=2),

@@ -27,8 +27,6 @@ HALF_V = V // 2
 BLOCKS = HALF_V // P
 MEAN, LARGEST, SMALLEST = 0, 1, 2
 
-PIECES = ((0, 256), (256, 512), (512, 768), (768, 896), (896, 1024))
-
 
 def tile_picked_pna_silu_e_kernel(
     tc, xT, w1, w2_words, w2_scales, w3_words, w3_scales, w4_words, w4_scales, offs, pos1, pos2, pos3, pos4, out
@@ -82,221 +80,223 @@ def tile_picked_pna_silu_e_kernel(
                     in_=scales_hbm[0, 4 * q : 4 * q + 4, :].bitcast(I32),
                 )
 
-        picked = [keep.tile([P, 2, S], BF16, name="picked%d" % u) for u in range(2)]
-        woven = [keep.tile([P, QUARTER_S, PACK], BF16, name="woven%d" % q, align_bytes=64) for q in range(4)]
+        picked = [[keep.tile([P, 2, QUARTER_S], BF16, name="picked%d_%d" % (u, q)) for q in range(4)] for u in range(2)]
+        woven = [keep.tile([P, QUARTER_S, PACK], BF16, name="woven%d" % q, tag="woven%d" % q, align_bytes=64) for q in range(4)]
 
-        def gather_x(j, c0, c1):
-            nc.vector.tensor_copy(out=picked[j // 2][:, j % 2, c0:c1], in_=x_plane[j][:].indirect(entries(offs_sb, c0, c1)))
+        def vector_gather(dst, window, offsets):
+            nc.vector.tensor_copy(out=dst, in_=window.indirect(offsets))
 
-        def weave(u, q):
-            nc.scalar.copy(
-                out=woven[q][:, :, 2 * u : 2 * u + 2],
-                in_=picked[u][:, :, q * QUARTER_S : (q + 1) * QUARTER_S].rearrange("p e c -> p c e"),
-            )
+        def scalar_gather(dst, window, offsets):
+            nc.scalar.activation(dst, window.indirect(offsets), ACT.Copy)
 
-        plane0_rounded = keep.tile([P, T], BF16, name="plane0_rounded")
-        nc.scalar.copy(out=plane0_rounded[:], in_=x_plane[0][:])
-        nc.scalar.activation(
-            picked[0][:, 0, S - QUARTER_S : S], plane0_rounded[:].indirect(entries(offs_sb, S - QUARTER_S, S)), ACT.Copy
-        )
-        gather_x(0, 0, S - QUARTER_S)
-        for c0 in range(0, S, HALF_S):
-            gather_x(1, c0, c0 + HALF_S)
-            for q in range(c0 // QUARTER_S, (c0 + HALF_S) // QUARTER_S):
-                weave(0, q)
-        gather_x(2, 0, S)
+        def gather_x(gather, j, q):
+            gather(picked[j // 2][q][:, j % 2, :], x_plane[j][:], entries(offs_sb, q * QUARTER_S, (q + 1) * QUARTER_S))
+
+        def weave(copy, u, q, c0=0, c1=QUARTER_S):
+            copy(out=woven[q][:, c0:c1, 2 * u : 2 * u + 2], in_=picked[u][q][:, :, c0:c1].rearrange("p e c -> p c e"))
+
+        for j in range(2):
+            for q in range(4):
+                gather_x(vector_gather if q < 2 else scalar_gather, j, q)
         for q in range(4):
-            gather_x(3, q * QUARTER_S, (q + 1) * QUARTER_S)
-            weave(1, q)
+            weave(nc.vector.tensor_copy if q < 2 else nc.scalar.copy, 0, q)
+        for q in range(4):
+            gather_x(vector_gather if q < 3 else scalar_gather, 2, q)
+        for q in range(4):
+            gather_x(vector_gather if q < 1 else scalar_gather, 3, q)
 
-        w_grouped = [
-            keep.tile([P, 2, P, PACK], BF16, name="w_grouped%d" % g, tag="w_grouped%d" % g, align_bytes=64)
-            for g in range(2)
-        ]
+        w_grouped = [keep.tile([P, 2, P, PACK], BF16, name="w_grouped0", tag="w_grouped0", align_bytes=64), None]
         x_codes = keep.tile([P, S], U32, name="x_codes", align_bytes=64)
         w_codes = keep.tile([P, H], U32, name="w_codes", align_bytes=64)
         w_scales = keep.tile([P, H], U8, name="w_scales", align_bytes=64)
-        x_scales = []
+        x_scales = {}
 
-        def group_w(g, m0, m1):
-            nc.vector.tensor_copy(
+        def group_w(copy, g, m0, m1):
+            copy(
                 out=w_grouped[g][:, :, m0:m1, :].rearrange("p e m j -> p m j e"),
                 in_=w_raw[:].rearrange("p j (m t) -> p m j t", t=PACK)[:, m0:m1, :, 2 * g : 2 * g + 2],
             )
 
-        def quantize_w(g):
+        def quantize_w(t0, t1):
             nc.vector.quantize_mx(
-                out=w_codes[:, 2 * g * P : 2 * (g + 1) * P].bitcast(FP8X4),
-                scales=w_scales[:, 2 * g * P : 2 * (g + 1) * P],
-                in_=w_grouped[g][:].rearrange("p e m j -> p (e m j)"),
+                out=w_codes[:, t0 * P : t1 * P].bitcast(FP8X4),
+                scales=w_scales[:, t0 * P : t1 * P],
+                in_=w_grouped[t0 // 2][:, t0 % 2 : t0 % 2 + t1 - t0, :, :].rearrange("p e m j -> p (e m j)"),
             )
 
-        def quantize_x(n):
-            c0, c1 = PIECES[n]
-            q = c0 // QUARTER_S
+        def quantize_x(q):
             nc.vector.quantize_mx(
-                out=x_codes[:, c0:c1].bitcast(FP8X4),
-                scales=x_scales[n],
-                in_=woven[q][:, c0 - q * QUARTER_S : c1 - q * QUARTER_S, :].rearrange("p s j -> p (s j)"),
+                out=x_codes[:, q * QUARTER_S : (q + 1) * QUARTER_S].bitcast(FP8X4),
+                scales=x_scales[q],
+                in_=woven[q][:].rearrange("p s j -> p (s j)"),
             )
 
-        group_w(0, 0, P)
-        first_scales = keep.tile([P, QUARTER_S], U8, name="first_scales", align_bytes=64)
-        x_scales.append(first_scales[:])
+        early_scales = keep.tile([P, 3 * QUARTER_S], U8, name="early_scales", align_bytes=64)
+        for q in range(3):
+            x_scales[q] = early_scales[:, q * QUARTER_S : (q + 1) * QUARTER_S]
+        weave(nc.vector.tensor_copy, 1, 1)
+        weave(nc.vector.tensor_copy, 1, 0)
+        quantize_x(1)
+        weave(nc.vector.tensor_copy, 1, 2)
         quantize_x(0)
-        quantize_w(0)
-        group_w(1, 0, P // 2)
-        group_w(1, P // 2, P)
-        late_scales = keep.tile([P, S - QUARTER_S], U8, name="late_scales", tag="w_grouped0", align_bytes=64)
-        for n in range(1, len(PIECES)):
-            x_scales.append(late_scales[:, PIECES[n][0] - QUARTER_S : PIECES[n][1] - QUARTER_S])
-            quantize_x(n)
-        quantize_w(1)
+        weave(nc.vector.tensor_copy, 1, 3)
+        quantize_x(2)
+        group_w(nc.scalar.copy, 0, 0, P)
+        quantize_w(0, 1)
+        quantize_w(1, 2)
+        late_scales = keep.tile([P, QUARTER_S], U8, name="late_scales", tag="w_grouped0", align_bytes=64)
+        x_scales[3] = late_scales[:]
+        quantize_x(3)
+        w_grouped[1] = keep.tile([P, 2, P, PACK], BF16, name="w_grouped_late", tag="woven3", align_bytes=64)
+        group_w(nc.vector.tensor_copy, 1, 0, P)
+        quantize_w(2, 4)
 
-        h_early = [keep.tile([P, S], F32, name="h%d" % t) for t in range(2)]
-        h_late = keep.tile([P, 2, S], F32, name="h_late")
-        h = [h_early[0][:], h_early[1][:], h_late[:, 0, :], h_late[:, 1, :]]
-
-        def product(dst, t, n):
-            c0, c1 = PIECES[n]
-            nc.tensor.matmul_mx(
-                out=dst,
-                lhsT=w_codes[:, t * P : (t + 1) * P].bitcast(FP8X4),
-                lhsT_scale=w_scales[:, t * P : (t + 1) * P],
-                rhs=x_codes[:, c0:c1].bitcast(FP8X4),
-                rhs_scale=x_scales[n],
-                start=True,
-                stop=True,
-            )
-
-        def silu(dst, src):
-            nc.scalar.activation(dst, src, ACT.Silu, bias=zero_bias[:])
+        h = [keep.tile([P, S], F32, name="h%d" % t) for t in range(PACK)]
 
         def h_stretch(bank_no, t, first, end):
-            c0, c1 = PIECES[first][0], PIECES[end - 1][1]
-            acc = bank(bank_no, [P, c1 - c0])
-            for n in range(first, end):
-                product(acc[:, PIECES[n][0] - c0 : PIECES[n][1] - c0], t, n)
-            silu(h[t][:, c0:c1], acc[:])
+            acc = bank(bank_no, [P, (end - first) * QUARTER_S])
+            for q in range(first, end):
+                nc.tensor.matmul_mx(
+                    out=acc[:, (q - first) * QUARTER_S : (q - first + 1) * QUARTER_S],
+                    lhsT=w_codes[:, t * P : (t + 1) * P].bitcast(FP8X4),
+                    lhsT_scale=w_scales[:, t * P : (t + 1) * P],
+                    rhs=x_codes[:, q * QUARTER_S : (q + 1) * QUARTER_S].bitcast(FP8X4),
+                    rhs_scale=x_scales[q],
+                    start=True,
+                    stop=True,
+                )
+            nc.scalar.activation(h[t][:, first * QUARTER_S : end * QUARTER_S], acc[:], ACT.Silu, bias=zero_bias[:])
 
-        last = len(PIECES) - 1
-        for n, bank_no in enumerate((4, 5, 6, 7, 3)):
-            h_stretch(bank_no, 0, n, n + 1)
-        h_stretch(6, 1, 0, 2)
-        h_stretch(7, 1, 2, last + 1)
-        for t, banks in ((2, (0, 1)), (3, (2, 4))):
+        h_stretch(4, 0, 0, 1)
+        h_stretch(5, 0, 1, 3)
+        h_stretch(6, 0, 3, 4)
+        for t, banks in ((1, (5, 6)), (2, (7, 0)), (3, (1, 4))):
             h_stretch(banks[0], t, 0, 2)
-            h_stretch(banks[1], t, 2, last)
-        last0, last1 = PIECES[last]
-        acc = bank(5, [P, 2, last1 - last0])
-        for e in range(2):
-            product(acc[:, e, :], 2 + e, last)
-        silu(h_late[:, :, last0:last1], acc[:])
-
-        fetched = [[keep.tile([P, 2, V], F32, name="fetched%d_%d" % (d, u)) for u in range(2)] for d in range(DEG)]
-        rounded = [keep.tile([P, V, PACK], BF16, name="rounded%d" % d) for d in range(DEG)]
-
-        def round_fetched(d, u):
-            nc.scalar.copy(out=rounded[d][:, :, 2 * u : 2 * u + 2], in_=fetched[d][u][:].rearrange("p e v -> p v e"))
+            h_stretch(banks[1], t, 2, 4)
 
         sum_t = [bank(b, [P, PACK, P]) for b in range(V // P)]
-        order = [(t, d) for t in range(2) for d in range(DEG)] + [(t, d) for d in range(DEG) for t in range(2, PACK)]
-        for n, (t, d) in enumerate(order):
-            dst = fetched[d][t // 2][:, t % 2, :]
-            nc.vector.tensor_copy(out=dst, in_=h[t].indirect(pos_sb[d][:]))
-            for b in range(V // P):
+        opened = set()
+        fetched = {}
+
+        def fetch(gather, t, d, v0, v1):
+            key = (d, t // 2, v0)
+            if key not in fetched:
+                fetched[key] = keep.tile([P, 2, v1 - v0], F32, name="fetched%d_%d_%d" % key)
+            dst = fetched[key][:, t % 2, :]
+            gather(dst, h[t][:], entries(pos_sb[d], v0, v1))
+            for b in range(v0 // P, v1 // P):
                 nc.tensor.matmul(
                     sum_t[b][:, t, :],
-                    lhsT=dst[:, b * P : (b + 1) * P],
+                    lhsT=dst[:, b * P - v0 : (b + 1) * P - v0],
                     rhs=ident[:],
                     is_transpose=True,
-                    start=(n == 0),
-                    stop=(n == len(order) - 1),
+                    start=(b not in opened),
+                    stop=(t == PACK - 1 and d == DEG - 1),
                 )
-            if t % 2 == 1:
-                round_fetched(d, t // 2)
+                opened.add(b)
 
-        flat = [r[:].rearrange("p v t -> p (v t)") for r in rounded]
-        hi_run, lo_run = flat[0], flat[0]
-        for d in range(1, DEG - 1):
-            hi_next = keep.tile([P, V * PACK], BF16, name="hi%d" % d)
-            lo_next = keep.tile([P, V * PACK], BF16, name="lo%d" % d)
-            nc.vector.tensor_tensor(out=hi_next[:], in0=hi_run, in1=flat[d], op=ALU.max)
-            nc.vector.tensor_tensor(out=lo_next[:], in0=lo_run, in1=flat[d], op=ALU.min)
-            hi_run, lo_run = hi_next[:], lo_next[:]
+        pairs = [
+            {op: keep.tile([P, 2, V, 2], BF16, name="pair%d_%d" % (c, n)) for n, op in enumerate((ALU.max, ALU.min))}
+            for c in range(2)
+        ]
+
+        def first_level(c, u, v0, v1):
+            for op in (ALU.max, ALU.min):
+                nc.vector.tensor_tensor(
+                    out=pairs[c][op][:, u, v0:v1, :],
+                    in0=fetched[2 * c, u, v0][:].rearrange("p e v -> p v e"),
+                    in1=fetched[2 * c + 1, u, v0][:].rearrange("p e v -> p v e"),
+                    op=op,
+                )
+
+        for d in range(3):
+            fetch(vector_gather, 0, d, 0, V)
+        fetch(scalar_gather, 1, 0, 0, V)
+        fetch(vector_gather, 0, 3, 0, V)
+        fetch(scalar_gather, 1, 1, 0, V)
+        fetch(vector_gather, 2, 0, 0, V)
+        fetch(scalar_gather, 1, 2, 0, V)
+        fetch(vector_gather, 2, 1, 0, V)
+        fetch(scalar_gather, 1, 3, 0, V)
+        first_level(0, 0, 0, V)
+        first_level(1, 0, 0, V)
+        fetch(scalar_gather, 3, 0, 0, V)
+        fetch(scalar_gather, 3, 1, 0, V)
+        first_level(0, 1, 0, V)
+        for half in range(2):
+            for d in range(2, DEG):
+                for t in range(2, PACK):
+                    fetch(scalar_gather, t, d, half * HALF_V, (half + 1) * HALF_V)
 
         means = []
-        for half in range(2):
+        mean_ts = []
+        for b in range(V // P):
+            mean_t = keep.tile([P, 2, P, 2], BF16, name="mean_t%d" % b, tag="mean_t%d" % b)
+            mean_ts.append(mean_t)
+
+        def round_sum(b):
+            nc.scalar.activation(
+                mean_ts[b][:], sum_t[b][:].rearrange("v (u e) p -> v u p e", e=2), ACT.Copy, scale=1.0 / DEG
+            )
+
+        def turn_back(half):
             back = bank(4 + half, [P, 2, HALF_V])
             for r in range(BLOCKS):
-                b = half * BLOCKS + r
-                mean_t = keep.tile([P, 2, P, 2], BF16, name="mean_t%d" % b, tag="mean_t%d" % b)
-                nc.scalar.activation(
-                    mean_t[:], sum_t[b][:].rearrange("v (u e) p -> v u p e", e=2), ACT.Copy, scale=1.0 / DEG
-                )
-                mean_words = mean_t[:].rearrange("v u p e -> v (u p e)").bitcast(F32)
+                mean_words = mean_ts[half * BLOCKS + r][:].rearrange("v u p e -> v (u p e)").bitcast(F32)
                 for u in range(2):
                     nc.tensor.transpose(back[:, u, r * P : (r + 1) * P], mean_words[:, u * P : (u + 1) * P], ident[:])
-            mean = keep.tile([P, HALF_V * PACK], BF16, name="mean%d" % half, tag="mean%d" % half, align_bytes=64)
+            mean = keep.tile([P, HALF_V * PACK], BF16, name="mean%d" % half, align_bytes=64)
             nc.scalar.copy(
                 out=mean[:].bitcast(F32).rearrange("p (v u) -> p v u", u=2),
                 in_=back[:].rearrange("p u v -> p v u"),
             )
             means.append(mean)
 
+        for b in range(V // P):
+            round_sum(b)
         for half in range(2):
-            cols = slice(half * HALF_V * PACK, (half + 1) * HALF_V * PACK)
-            extremes = keep.tile(
-                [P, 2, HALF_V * PACK], BF16, name="extremes%d" % half, tag=("extremes0", "mean0")[half], align_bytes=64
-            )
-            hi, lo = extremes[:, 0, :], extremes[:, 1, :]
-            nc.vector.tensor_tensor(out=hi, in0=hi_run[:, cols], in1=flat[DEG - 1][:, cols], op=ALU.max)
-            nc.vector.tensor_tensor(out=lo, in0=lo_run[:, cols], in1=flat[DEG - 1][:, cols], op=ALU.min)
+            turn_back(half)
 
-            z_codes = keep.tile([P, 3 * HALF_V], U32, name="z_codes%d" % half, align_bytes=64)
-            z_scales = keep.tile([P, 3 * HALF_V], U8, name="z_scales%d" % half, align_bytes=64)
+        z_codes = [keep.tile([P, 3 * HALF_V], U32, name="z_codes%d" % half, align_bytes=64) for half in range(2)]
+        z_scales = [keep.tile([P, 3 * HALF_V], U8, name="z_scales%d" % half, align_bytes=64) for half in range(2)]
+        res = [[bank(n, [P, HALF_V]) for n in banks] for banks in ((6, 7), (0, 1))]
 
-            def quantize_z(c0, z):
-                c1 = c0 + z.shape[1] // PACK
-                nc.vector.quantize_mx(out=z_codes[:, c0:c1].bitcast(FP8X4), scales=z_scales[:, c0:c1], in_=z)
+        def multiply(half, a, z):
+            z_cols = slice(a * HALF_V, (a + 1) * HALF_V)
+            nc.vector.quantize_mx(out=z_codes[half][:, z_cols].bitcast(FP8X4), scales=z_scales[half][:, z_cols], in_=z)
+            for m in range(N // P):
+                nc.tensor.matmul_mx(
+                    out=res[half][m][:],
+                    lhsT=wq_words[a][:, m * 2 * P : (m + 1) * 2 * P].bitcast(FP4X4),
+                    lhsT_scale=wq_scales[:, a * N + m * P : a * N + (m + 1) * P],
+                    rhs=z_codes[half][:, z_cols].bitcast(FP8X4),
+                    rhs_scale=z_scales[half][:, z_cols],
+                    start=(a == LARGEST),
+                    stop=(a == MEAN),
+                )
 
-            quantize_z(MEAN * HALF_V, means[half][:])
-            if half == 0:
-                quantize_z(LARGEST * HALF_V, extremes[:].rearrange("p a c -> p (a c)"))
-            else:
-                quantize_z(LARGEST * HALF_V, hi)
-                for r in range(BLOCKS):
-                    quantize_z(SMALLEST * HALF_V + r * P, lo[:, r * P * PACK : (r + 1) * P * PACK])
-
-            res = [bank(n, [P, P]) for n in ((0, 1, 6, 7), (2, 3, 4, 5))[half]]
-            for a in (MEAN, LARGEST, SMALLEST):
-                for r in range(BLOCKS):
-                    z_cols = slice(a * HALF_V + r * P, a * HALF_V + (r + 1) * P)
-                    for m in range(N // P):
-                        nc.tensor.matmul_mx(
-                            out=res[BLOCKS * m + r][:],
-                            lhsT=wq_words[a][:, m * 2 * P : (m + 1) * 2 * P].bitcast(FP4X4),
-                            lhsT_scale=wq_scales[:, a * N + m * P : a * N + (m + 1) * P],
-                            rhs=z_codes[:, z_cols].bitcast(FP8X4),
-                            rhs_scale=z_scales[:, z_cols],
-                            start=(a == MEAN),
-                            stop=(a == SMALLEST),
-                        )
-
-            staged = [
-                keep.tile([P, HALF_V], F32, name="staged%d_%d" % (m, half), tag="mean_t%d" % (BLOCKS * (1 - half) + m))
-                for m in range(N // P)
-            ]
-            if half == 0:
-                for m in range(N // P):
-                    for r in range(BLOCKS):
-                        nc.scalar.copy(out=staged[m][:, r * P : (r + 1) * P], in_=res[BLOCKS * m + r][:])
-                    nc.sync.dma_start(out=out[m * P : (m + 1) * P, 0:HALF_V], in_=staged[m][:])
-            else:
-                for r in range(BLOCKS):
-                    for m in range(N // P):
-                        copy, queue = (nc.scalar.copy, nc.scalar) if m == r else (nc.vector.tensor_copy, nc.sync)
-                        block = staged[m][:, r * P : (r + 1) * P]
-                        copy(out=block, in_=res[BLOCKS * m + r][:])
-                        v0 = HALF_V + r * P
-                        queue.dma_start(out=out[m * P : (m + 1) * P, v0 : v0 + P], in_=block)
+        for half in range(2):
+            v0, v1 = half * HALF_V, (half + 1) * HALF_V
+            first_level(1, 1, v0, v1)
+            extremes = keep.tile([P, 2, HALF_V, 2, 2], BF16, name="extremes%d" % half, align_bytes=64)
+            for n, op in enumerate((ALU.max, ALU.min)):
+                nc.vector.tensor_tensor(
+                    out=extremes[:, n, :, :, :],
+                    in0=pairs[0][op][:, :, v0:v1, :].rearrange("p u v e -> p v u e"),
+                    in1=pairs[1][op][:, :, v0:v1, :].rearrange("p u v e -> p v u e"),
+                    op=op,
+                )
+            multiply(half, LARGEST, extremes[:, 0, :, :, :].rearrange("p v u e -> p (v u e)"))
+            multiply(half, SMALLEST, extremes[:, 1, :, :, :].rearrange("p v u e -> p (v u e)"))
+        for half in range(2):
+            multiply(half, MEAN, means[half][:])
+        for half in range(2):
+            v0, v1 = half * HALF_V, (half + 1) * HALF_V
+            for m in range(N // P):
+                staged = keep.tile([P, HALF_V], F32, name="staged%d_%d" % (m, half))
+                if m == 0:
+                    nc.vector.tensor_copy(out=staged[:], in_=res[half][m][:])
+                else:
+                    nc.scalar.copy(out=staged[:], in_=res[half][m][:])
+                queue = nc.scalar if (half == 1 and m == 1) else nc.sync
+                queue.dma_start(out=out[m * P : (m + 1) * P, v0:v1], in_=staged[:])

@@ -151,7 +151,8 @@ def tile_picked_pna_silu_e_kernel(
         group_w(nc.vector.tensor_copy, 1, 0, P)
         quantize_w(2, 4)
 
-        h = [keep.tile([P, S], F32, name="h%d" % t) for t in range(PACK)]
+        h = {}
+        h_tags = ("h0", "h1", "fetched0_0_0", "fetched1_0_0")
 
         def h_stretch(bank_no, t, first, end):
             acc = bank(bank_no, [P, (end - first) * QUARTER_S])
@@ -165,14 +166,20 @@ def tile_picked_pna_silu_e_kernel(
                     start=True,
                     stop=True,
                 )
-            nc.scalar.activation(h[t][:, first * QUARTER_S : end * QUARTER_S], acc[:], ACT.Silu, bias=zero_bias[:])
 
-        h_stretch(4, 0, 0, 1)
-        h_stretch(5, 0, 1, 3)
-        h_stretch(6, 0, 3, 4)
-        for t, banks in ((1, (5, 6)), (2, (7, 0)), (3, (1, 4))):
-            h_stretch(banks[0], t, 0, 2)
-            h_stretch(banks[1], t, 2, 4)
+            def silu():
+                if t not in h:
+                    h[t] = keep.tile([P, S], F32, name="h%d" % t, tag=h_tags[t], align_bytes=64)
+                nc.scalar.activation(h[t][:, first * QUARTER_S : end * QUARTER_S], acc[:], ACT.Silu, bias=zero_bias[:])
+
+            return silu
+
+        h_stretch(4, 0, 0, 1)()
+        h_stretch(5, 0, 1, 3)()
+        h_stretch(6, 0, 3, 4)()
+        h_stretch(7, 1, 0, 2)()
+        h_stretch(4, 1, 2, 4)()
+        late_silus = [h_stretch(5, 2, 0, 2), h_stretch(6, 2, 2, 4), h_stretch(7, 3, 0, 2), h_stretch(4, 3, 2, 4)]
 
         sum_t = [bank(b, [P, PACK, P]) for b in range(V // P)]
         opened = set()
@@ -181,7 +188,8 @@ def tile_picked_pna_silu_e_kernel(
         def fetch(gather, t, d, v0, v1):
             key = (d, t // 2, v0)
             if key not in fetched:
-                fetched[key] = keep.tile([P, 2, v1 - v0], F32, name="fetched%d_%d_%d" % key)
+                tag = "fetched%d_%d_%d" % ((d, 1, 0) if key == (DEG - 1, 1, HALF_V) else key)
+                fetched[key] = keep.tile([P, 2, v1 - v0], F32, name="fetched%d_%d_%d" % key, tag=tag, align_bytes=64)
             dst = fetched[key][:, t % 2, :]
             gather(dst, h[t][:], entries(pos_sb[d], v0, v1))
             for b in range(v0 // P, v1 // P):
@@ -209,75 +217,96 @@ def tile_picked_pna_silu_e_kernel(
                     op=op,
                 )
 
-        for d in range(3):
-            fetch(vector_gather, 0, d, 0, V)
-        fetch(scalar_gather, 1, 0, 0, V)
-        fetch(vector_gather, 0, 3, 0, V)
-        fetch(scalar_gather, 1, 1, 0, V)
-        fetch(vector_gather, 2, 0, 0, V)
-        fetch(scalar_gather, 1, 2, 0, V)
-        fetch(vector_gather, 2, 1, 0, V)
-        fetch(scalar_gather, 1, 3, 0, V)
-        first_level(0, 0, 0, V)
-        first_level(1, 0, 0, V)
-        fetch(scalar_gather, 3, 0, 0, V)
-        fetch(scalar_gather, 3, 1, 0, V)
-        first_level(0, 1, 0, V)
-        for half in range(2):
-            for d in range(2, DEG):
-                for t in range(2, PACK):
-                    fetch(scalar_gather, t, d, half * HALF_V, (half + 1) * HALF_V)
+        rounded = {}
 
-        means = []
-        mean_ts = []
-        for b in range(V // P):
-            mean_t = keep.tile([P, 2, P, 2], BF16, name="mean_t%d" % b, tag="mean_t%d" % b)
-            mean_ts.append(mean_t)
+        def round_fetched(d):
+            tag = "fetched2_0_0" if d == DEG - 1 else "rounded%d" % d
+            rounded[d] = keep.tile([P, V, 2], BF16, name="rounded%d" % d, tag=tag, align_bytes=64)
+            nc.gpsimd.tensor_scalar(
+                rounded[d][:], fetched[d, 0, 0][:].rearrange("p e v -> p v e"), 1.0, 0.0, ALU.mult, ALU.add
+            )
+
+        def first_level_rounded(c):
+            for op in (ALU.max, ALU.min):
+                nc.vector.tensor_tensor(out=pairs[c][op][:, 0, :, :], in0=rounded[2 * c][:], in1=rounded[2 * c + 1][:], op=op)
+
+        for d in range(DEG - 1):
+            fetch(vector_gather, 0, d, 0, V)
+            fetch(scalar_gather, 1, d, 0, V)
+            round_fetched(d)
+        for silu in late_silus:
+            silu()
+        fetch(vector_gather, 0, 3, 0, V)
+        fetch(vector_gather, 1, 3, 0, V)
+        round_fetched(3)
+        fetch(vector_gather, 2, 0, 0, V)
+        fetch(vector_gather, 3, 0, 0, V)
+        fetch(scalar_gather, 2, 1, 0, V)
+        fetch(scalar_gather, 3, 1, 0, V)
+        first_level_rounded(0)
+        first_level_rounded(1)
+        first_level(0, 1, 0, V)
+
+        mean_t = [keep.tile([P, 2, P, 2], BF16, name="mean_t%d" % b) for b in range(V // P)]
 
         def round_sum(b):
             nc.scalar.activation(
-                mean_ts[b][:], sum_t[b][:].rearrange("v (u e) p -> v u p e", e=2), ACT.Copy, scale=1.0 / DEG
+                mean_t[b][:], sum_t[b][:].rearrange("v (u e) p -> v u p e", e=2), ACT.Copy, scale=1.0 / DEG
             )
 
-        def turn_back(half):
-            back = bank(4 + half, [P, 2, HALF_V])
-            for r in range(BLOCKS):
-                mean_words = mean_ts[half * BLOCKS + r][:].rearrange("v u p e -> v (u p e)").bitcast(F32)
+        def turn_back(bank_no, b0, b1):
+            back = bank(bank_no, [P, 2, (b1 - b0) * P])
+            for b in range(b0, b1):
+                mean_words = mean_t[b][:].rearrange("v u p e -> v (u p e)").bitcast(F32)
                 for u in range(2):
-                    nc.tensor.transpose(back[:, u, r * P : (r + 1) * P], mean_words[:, u * P : (u + 1) * P], ident[:])
-            mean = keep.tile([P, HALF_V * PACK], BF16, name="mean%d" % half, align_bytes=64)
+                    nc.tensor.transpose(
+                        back[:, u, (b - b0) * P : (b - b0 + 1) * P], mean_words[:, u * P : (u + 1) * P], ident[:]
+                    )
+            mean = keep.tile([P, (b1 - b0) * P * PACK], BF16, name="mean%d" % b0, tag=h_tags[3] if b0 == 0 else "mean%d" % b0, align_bytes=64)
             nc.scalar.copy(
                 out=mean[:].bitcast(F32).rearrange("p (v u) -> p v u", u=2),
                 in_=back[:].rearrange("p u v -> p v u"),
             )
-            means.append(mean)
+            return mean
 
-        for b in range(V // P):
-            round_sum(b)
-        for half in range(2):
-            turn_back(half)
+        def fetch_last_lists(half, d):
+            for t in range(2, PACK):
+                fetch(scalar_gather, t, d, half * HALF_V, (half + 1) * HALF_V)
 
-        z_codes = [keep.tile([P, 3 * HALF_V], U32, name="z_codes%d" % half, align_bytes=64) for half in range(2)]
-        z_scales = [keep.tile([P, 3 * HALF_V], U8, name="z_scales%d" % half, align_bytes=64) for half in range(2)]
-        res = [[bank(n, [P, HALF_V]) for n in banks] for banks in ((6, 7), (0, 1))]
+        fetch_last_lists(0, 2)
+        fetch_last_lists(0, 3)
+        first_level(1, 1, 0, HALF_V)
+        fetch_last_lists(1, 2)
+        round_sum(0)
+        round_sum(1)
+        fetch_last_lists(1, 3)
+        first_mean = turn_back(4, 0, 2)
+        round_sum(2)
+        round_sum(3)
+        last_means = [turn_back(5, 2, 3), turn_back(4, 3, 4)]
 
-        def multiply(half, a, z):
-            z_cols = slice(a * HALF_V, (a + 1) * HALF_V)
-            nc.vector.quantize_mx(out=z_codes[half][:, z_cols].bitcast(FP8X4), scales=z_scales[half][:, z_cols], in_=z)
-            for m in range(N // P):
-                nc.tensor.matmul_mx(
-                    out=res[half][m][:],
-                    lhsT=wq_words[a][:, m * 2 * P : (m + 1) * 2 * P].bitcast(FP4X4),
-                    lhsT_scale=wq_scales[:, a * N + m * P : a * N + (m + 1) * P],
-                    rhs=z_codes[half][:, z_cols].bitcast(FP8X4),
-                    rhs_scale=z_scales[half][:, z_cols],
-                    start=(a == LARGEST),
-                    stop=(a == MEAN),
-                )
+        z_codes = [keep.tile([P, V], U32, name="z_codes%d" % a, align_bytes=64) for a in range(3)]
+        z_scales = [keep.tile([P, V], U8, name="z_scales%d" % a, align_bytes=64) for a in range(3)]
+        stretches = ((0, HALF_V, (6, 7)), (HALF_V, HALF_V + P, (0, 1)), (HALF_V + P, V, (2, 3)))
+        res = {v0: [bank(n, [P, v1 - v0]) for n in banks] for v0, v1, banks in stretches}
 
-        for half in range(2):
+        def multiply(a, c0, c1, z):
+            nc.vector.quantize_mx(out=z_codes[a][:, c0:c1].bitcast(FP8X4), scales=z_scales[a][:, c0:c1], in_=z)
+            for v0, v1, banks in stretches:
+                if c0 <= v0 and v1 <= c1:
+                    for m in range(N // P):
+                        nc.tensor.matmul_mx(
+                            out=res[v0][m][:],
+                            lhsT=wq_words[a][:, m * 2 * P : (m + 1) * 2 * P].bitcast(FP4X4),
+                            lhsT_scale=wq_scales[:, a * N + m * P : a * N + (m + 1) * P],
+                            rhs=z_codes[a][:, v0:v1].bitcast(FP8X4),
+                            rhs_scale=z_scales[a][:, v0:v1],
+                            start=(a == LARGEST),
+                            stop=(a == MEAN),
+                        )
+
+        def second_level(half):
             v0, v1 = half * HALF_V, (half + 1) * HALF_V
-            first_level(1, 1, v0, v1)
             extremes = keep.tile([P, 2, HALF_V, 2, 2], BF16, name="extremes%d" % half, align_bytes=64)
             for n, op in enumerate((ALU.max, ALU.min)):
                 nc.vector.tensor_tensor(
@@ -286,17 +315,21 @@ def tile_picked_pna_silu_e_kernel(
                     in1=pairs[1][op][:, :, v0:v1, :].rearrange("p u v e -> p v u e"),
                     op=op,
                 )
-            multiply(half, LARGEST, extremes[:, 0, :, :, :].rearrange("p v u e -> p (v u e)"))
-            multiply(half, SMALLEST, extremes[:, 1, :, :, :].rearrange("p v u e -> p (v u e)"))
-        for half in range(2):
-            multiply(half, MEAN, means[half][:])
-        for half in range(2):
-            v0, v1 = half * HALF_V, (half + 1) * HALF_V
+            multiply(LARGEST, v0, v1, extremes[:, 0, :, :, :].rearrange("p v u e -> p (v u e)"))
+            multiply(SMALLEST, v0, v1, extremes[:, 1, :, :, :].rearrange("p v u e -> p (v u e)"))
+
+        def store(v0, v1, copies, queues):
             for m in range(N // P):
-                staged = keep.tile([P, HALF_V], F32, name="staged%d_%d" % (m, half))
-                if m == 0:
-                    nc.vector.tensor_copy(out=staged[:], in_=res[half][m][:])
-                else:
-                    nc.scalar.copy(out=staged[:], in_=res[half][m][:])
-                queue = nc.scalar if (half == 1 and m == 1) else nc.sync
-                queue.dma_start(out=out[m * P : (m + 1) * P, v0:v1], in_=staged[:])
+                staged = keep.tile([P, v1 - v0], F32, name="staged%d_%d" % (m, v0))
+                copies[m](out=staged[:], in_=res[v0][m][:])
+                queues[m].dma_start(out=out[m * P : (m + 1) * P, v0:v1], in_=staged[:])
+
+        second_level(0)
+        first_level(1, 1, HALF_V, V)
+        multiply(MEAN, 0, HALF_V, first_mean[:])
+        store(0, HALF_V, (nc.scalar.copy, nc.scalar.copy), (nc.sync, nc.sync))
+        second_level(1)
+        for r in range(BLOCKS):
+            multiply(MEAN, HALF_V + r * P, HALF_V + (r + 1) * P, last_means[r][:])
+        store(HALF_V, HALF_V + P, (nc.scalar.copy, nc.vector.tensor_copy), (nc.sync, nc.sync))
+        store(HALF_V + P, V, (nc.vector.tensor_copy, nc.scalar.copy), (nc.sync, nc.scalar))

@@ -247,7 +247,7 @@ def tile_picked_pna_silu_e_kernel(
         first_level_rounded(1)
         first_level(0, 1, 0, V)
 
-        mean_t = [keep.tile([P, 2, P, 2], BF16, name="mean_t%d" % b) for b in range(V // P)]
+        mean_t = [keep.tile([P, 2, P, 2], BF16, name="mean_t%d" % b, tag="mean_t%d" % b) for b in range(V // P)]
 
         def round_sum(b):
             nc.scalar.activation(
@@ -302,34 +302,41 @@ def tile_picked_pna_silu_e_kernel(
                             rhs=z_codes[a][:, v0:v1].bitcast(FP8X4),
                             rhs_scale=z_scales[a][:, v0:v1],
                             start=(a == LARGEST),
-                            stop=(a == MEAN),
+                            stop=(a == (SMALLEST if v0 == HALF_V else MEAN)),
                         )
 
-        def second_level(half):
-            v0, v1 = half * HALF_V, (half + 1) * HALF_V
-            extremes = keep.tile([P, 2, HALF_V, 2, 2], BF16, name="extremes%d" % half, align_bytes=64)
-            for n, op in enumerate((ALU.max, ALU.min)):
-                nc.vector.tensor_tensor(
-                    out=extremes[:, n, :, :, :],
-                    in0=pairs[0][op][:, :, v0:v1, :].rearrange("p u v e -> p v u e"),
-                    in1=pairs[1][op][:, :, v0:v1, :].rearrange("p u v e -> p v u e"),
-                    op=op,
-                )
-            multiply(LARGEST, v0, v1, extremes[:, 0, :, :, :].rearrange("p v u e -> p (v u e)"))
-            multiply(SMALLEST, v0, v1, extremes[:, 1, :, :, :].rearrange("p v u e -> p (v u e)"))
+        def second_level(op, v0, v1):
+            extreme = keep.tile([P, v1 - v0, 2, 2], BF16, name="extreme%d_%d" % (op == ALU.max, v0), align_bytes=64)
+            nc.vector.tensor_tensor(
+                out=extreme[:],
+                in0=pairs[0][op][:, :, v0:v1, :].rearrange("p u v e -> p v u e"),
+                in1=pairs[1][op][:, :, v0:v1, :].rearrange("p u v e -> p v u e"),
+                op=op,
+            )
+            return extreme[:].rearrange("p v u e -> p (v u e)")
 
         def store(v0, v1, copies, queues):
             for m in range(N // P):
-                staged = keep.tile([P, v1 - v0], F32, name="staged%d_%d" % (m, v0))
+                tag = "mean_t%d" % (BLOCKS + 1 - m) if v0 == 0 else "staged%d_%d" % (m, v0)
+                staged = keep.tile([P, v1 - v0], F32, name="staged%d_%d" % (m, v0), tag=tag)
                 copies[m](out=staged[:], in_=res[v0][m][:])
                 queues[m].dma_start(out=out[m * P : (m + 1) * P, v0:v1], in_=staged[:])
 
-        second_level(0)
+        largest = second_level(ALU.max, 0, HALF_V)
+        smallest = second_level(ALU.min, 0, HALF_V)
+        multiply(LARGEST, 0, HALF_V, largest)
+        multiply(SMALLEST, 0, HALF_V, smallest)
         first_level(1, 1, HALF_V, V)
         multiply(MEAN, 0, HALF_V, first_mean[:])
-        store(0, HALF_V, (nc.scalar.copy, nc.scalar.copy), (nc.sync, nc.sync))
-        second_level(1)
+        blocks = [(HALF_V + r * P, HALF_V + (r + 1) * P) for r in range(BLOCKS)]
+        largest = second_level(ALU.max, HALF_V, V)
+        smallest = [second_level(ALU.min, *blocks[0])]
+        multiply(LARGEST, HALF_V, V, largest)
+        multiply(MEAN, *blocks[0], last_means[0][:])
+        smallest.append(second_level(ALU.min, *blocks[1]))
         for r in range(BLOCKS):
-            multiply(MEAN, HALF_V + r * P, HALF_V + (r + 1) * P, last_means[r][:])
-        store(HALF_V, HALF_V + P, (nc.scalar.copy, nc.vector.tensor_copy), (nc.sync, nc.sync))
-        store(HALF_V + P, V, (nc.vector.tensor_copy, nc.scalar.copy), (nc.sync, nc.scalar))
+            multiply(SMALLEST, *blocks[r], smallest[r])
+        multiply(MEAN, *blocks[1], last_means[1][:])
+        store(0, HALF_V, (nc.scalar.copy, nc.scalar.copy), (nc.sync, nc.sync))
+        store(*blocks[0], (nc.scalar.copy, nc.vector.tensor_copy), (nc.sync, nc.sync))
+        store(*blocks[1], (nc.vector.tensor_copy, nc.scalar.copy), (nc.sync, nc.scalar))

@@ -102,8 +102,10 @@ def tile_picked_pna_silu_e_kernel(
             weave(nc.vector.tensor_copy if q < 2 else nc.scalar.copy, 0, q)
         for q in range(4):
             gather_x(vector_gather if q < 3 else scalar_gather, 2, q)
-        for q in range(4):
-            gather_x(vector_gather if q < 1 else scalar_gather, 3, q)
+        nc.vector.tensor_copy(out=woven[0][:, :, 2], in_=picked[1][0][:, 0, :])
+        vector_gather(woven[0][:, :, 3], x_plane[3][:], entries(offs_sb, 0, QUARTER_S))
+        for q in range(1, 4):
+            gather_x(scalar_gather, 3, q)
 
         w_grouped = [keep.tile([P, 2, P, PACK], BF16, name="w_grouped0", tag="w_grouped0", align_bytes=64), None]
         x_codes = keep.tile([P, S], U32, name="x_codes", align_bytes=64)
@@ -131,38 +133,36 @@ def tile_picked_pna_silu_e_kernel(
                 in_=woven[q][:].rearrange("p s j -> p (s j)"),
             )
 
-        early_scales = keep.tile([P, 3 * QUARTER_S], U8, name="early_scales", align_bytes=64)
-        for q in range(3):
+        early_scales = keep.tile([P, S], U8, name="early_scales", align_bytes=64)
+        for q in range(4):
             x_scales[q] = early_scales[:, q * QUARTER_S : (q + 1) * QUARTER_S]
         weave(nc.vector.tensor_copy, 1, 1)
-        weave(nc.vector.tensor_copy, 1, 0)
-        quantize_x(1)
-        weave(nc.vector.tensor_copy, 1, 2)
         quantize_x(0)
+        weave(nc.vector.tensor_copy, 1, 2)
+        quantize_x(1)
         weave(nc.vector.tensor_copy, 1, 3)
         quantize_x(2)
+        quantize_x(3)
         group_w(nc.scalar.copy, 0, 0, P)
         quantize_w(0, 1)
         quantize_w(1, 2)
-        late_scales = keep.tile([P, QUARTER_S], U8, name="late_scales", tag="w_grouped0", align_bytes=64)
-        x_scales[3] = late_scales[:]
-        quantize_x(3)
-        w_grouped[1] = keep.tile([P, 2, P, PACK], BF16, name="w_grouped_late", tag="woven3", align_bytes=64)
+        w_grouped[1] = keep.tile([P, 2, P, PACK], BF16, name="w_grouped_late", tag="w_grouped0", align_bytes=64)
         group_w(nc.vector.tensor_copy, 1, 0, P)
         quantize_w(2, 4)
 
         h = {}
-        h_tags = ("h0", "h1", "fetched0_0_0", "fetched1_0_0")
+        h_tags = ("h0", "h1", "h2", "fetched0_0_0")
 
-        def h_stretch(bank_no, t, first, end):
-            acc = bank(bank_no, [P, (end - first) * QUARTER_S])
-            for q in range(first, end):
+        def h_stretch(bank_no, t, c0, c1):
+            acc = bank(bank_no, [P, c1 - c0])
+            for n0 in range(c0, c1, QUARTER_S):
+                n1 = min(n0 + QUARTER_S, c1)
                 nc.tensor.matmul_mx(
-                    out=acc[:, (q - first) * QUARTER_S : (q - first + 1) * QUARTER_S],
+                    out=acc[:, n0 - c0 : n1 - c0],
                     lhsT=w_codes[:, t * P : (t + 1) * P].bitcast(FP8X4),
                     lhsT_scale=w_scales[:, t * P : (t + 1) * P],
-                    rhs=x_codes[:, q * QUARTER_S : (q + 1) * QUARTER_S].bitcast(FP8X4),
-                    rhs_scale=x_scales[q],
+                    rhs=x_codes[:, n0:n1].bitcast(FP8X4),
+                    rhs_scale=early_scales[:, n0:n1],
                     start=True,
                     stop=True,
                 )
@@ -170,29 +170,34 @@ def tile_picked_pna_silu_e_kernel(
             def silu():
                 if t not in h:
                     h[t] = keep.tile([P, S], F32, name="h%d" % t, tag=h_tags[t], align_bytes=64)
-                nc.scalar.activation(h[t][:, first * QUARTER_S : end * QUARTER_S], acc[:], ACT.Silu, bias=zero_bias[:])
+                nc.scalar.activation(h[t][:, c0:c1], acc[:], ACT.Silu, bias=zero_bias[:])
 
             return silu
 
-        h_stretch(4, 0, 0, 1)()
-        h_stretch(5, 0, 1, 3)()
-        h_stretch(6, 0, 3, 4)()
-        h_stretch(7, 1, 0, 2)()
-        h_stretch(4, 1, 2, 4)()
-        late_silus = [h_stretch(5, 2, 0, 2), h_stretch(6, 2, 2, 4), h_stretch(7, 3, 0, 2), h_stretch(4, 3, 2, 4)]
+        for n, (c0, c1) in enumerate(((0, 128), (128, 384), (384, 640), (640, S))):
+            h_stretch(4 + n, 0, c0, c1)()
+        h_stretch(4, 1, 0, HALF_S)()
+        h_stretch(5, 1, HALF_S, S)()
+        late_silus = [h_stretch((6 + n) % 4 + 4, 2 + n // 2, n % 2 * HALF_S, (n % 2 + 1) * HALF_S) for n in range(4)]
 
         sum_t = [bank(b, [P, PACK, P]) for b in range(V // P)]
         opened = set()
         fetched = {}
 
-        def fetch(gather, t, d, v0, v1):
+        def fetch(gather, t, d, v0, v1, c0=None, c1=None):
             key = (d, t // 2, v0)
+            if key == (DEG - 1, 1, 0) and key not in fetched:
+                rows = keep.tile([P, 3, HALF_V], F32, name="fetched_last", align_bytes=64)
+                fetched[key] = rows[:, 1:3, :]
+                fetched[DEG - 1, 1, HALF_V] = rows[:, 0:2, :]
             if key not in fetched:
-                tag = "fetched%d_%d_%d" % ((d, 1, 0) if key == (DEG - 1, 1, HALF_V) else key)
-                fetched[key] = keep.tile([P, 2, v1 - v0], F32, name="fetched%d_%d_%d" % key, tag=tag, align_bytes=64)
+                tile = keep.tile([P, 2, v1 - v0], F32, name="fetched%d_%d_%d" % key, tag="fetched%d_%d_%d" % key, align_bytes=64)
+                fetched[key] = tile[:]
+            if c0 is None:
+                c0, c1 = v0, v1
             dst = fetched[key][:, t % 2, :]
-            gather(dst, h[t][:], entries(pos_sb[d], v0, v1))
-            for b in range(v0 // P, v1 // P):
+            gather(dst[:, c0 - v0 : c1 - v0], h[t][:], entries(pos_sb[d], c0, c1))
+            for b in range(c0 // P, c1 // P):
                 nc.tensor.matmul(
                     sum_t[b][:, t, :],
                     lhsT=dst[:, b * P - v0 : (b + 1) * P - v0],
@@ -203,49 +208,69 @@ def tile_picked_pna_silu_e_kernel(
                 )
                 opened.add(b)
 
-        pairs = [
-            {op: keep.tile([P, 2, V, 2], BF16, name="pair%d_%d" % (c, n)) for n, op in enumerate((ALU.max, ALU.min))}
-            for c in range(2)
-        ]
+        pairs = {1: keep.tile([P, 8, HALF_V, 2], BF16, name="pairs1", align_bytes=64)}
+        EXTREMES = (ALU.max, ALU.min)
 
-        def first_level(c, u, v0, v1):
-            for op in (ALU.max, ALU.min):
+        def row_of(c, u, n, half):
+            if c == 1 and u == 1:
+                return 4 + 2 * half + n
+            return 4 * u + 2 * n + half
+
+        def first_level(c, v0, v1):
+            for n, op in enumerate(EXTREMES):
+                row = row_of(c, 1, n, v0 // HALF_V)
                 nc.vector.tensor_tensor(
-                    out=pairs[c][op][:, u, v0:v1, :],
-                    in0=fetched[2 * c, u, v0][:].rearrange("p e v -> p v e"),
-                    in1=fetched[2 * c + 1, u, v0][:].rearrange("p e v -> p v e"),
+                    out=pairs[c][:, row : row + (v1 - v0) // HALF_V, :, :].rearrange("p r v e -> p (r v) e"),
+                    in0=fetched[2 * c, 1, v0].rearrange("p e v -> p v e"),
+                    in1=fetched[2 * c + 1, 1, v0].rearrange("p e v -> p v e"),
                     op=op,
                 )
 
         rounded = {}
 
         def round_fetched(d):
-            tag = "fetched2_0_0" if d == DEG - 1 else "rounded%d" % d
-            rounded[d] = keep.tile([P, V, 2], BF16, name="rounded%d" % d, tag=tag, align_bytes=64)
-            nc.gpsimd.tensor_scalar(
-                rounded[d][:], fetched[d, 0, 0][:].rearrange("p e v -> p v e"), 1.0, 0.0, ALU.mult, ALU.add
+            if d == DEG - 1:
+                pairs[0] = keep.tile([P, 8, HALF_V, 2], BF16, name="pairs0", tag="fetched2_0_0", align_bytes=64)
+            c, row = ((1, 2), (1, 0), (1, 4), (0, 5))[d]
+            rounded[d] = pairs[c][:, row : row + 2, :, :].rearrange("p r v e -> p (r v) e")
+            if d == 0:
+                for e in range(2):
+                    nc.gpsimd.tensor_scalar(rounded[d][:, :, e], fetched[d, 0, 0][:, e, :], 1.0, 0.0, ALU.mult, ALU.add)
+            else:
+                nc.gpsimd.tensor_scalar(
+                    rounded[d], fetched[d, 0, 0].rearrange("p e v -> p v e"), 1.0, 0.0, ALU.mult, ALU.add
+                )
+
+        def first_level_rounded(c, n, d0, d1):
+            row = row_of(c, 0, n, 0)
+            nc.vector.tensor_tensor(
+                out=pairs[c][:, row : row + 2, :, :].rearrange("p r v e -> p (r v) e"),
+                in0=rounded[d0],
+                in1=rounded[d1],
+                op=EXTREMES[n],
             )
 
-        def first_level_rounded(c):
-            for op in (ALU.max, ALU.min):
-                nc.vector.tensor_tensor(out=pairs[c][op][:, 0, :, :], in0=rounded[2 * c][:], in1=rounded[2 * c + 1][:], op=op)
-
-        for d in range(DEG - 1):
+        for d in range(2):
             fetch(vector_gather, 0, d, 0, V)
             fetch(scalar_gather, 1, d, 0, V)
             round_fetched(d)
+        fetch(vector_gather, 0, 2, 0, V)
+        fetch(scalar_gather, 1, 2, 0, V)
+        fetch(vector_gather, 0, 3, 0, V)
+        round_fetched(2)
         for silu in late_silus:
             silu()
-        fetch(vector_gather, 0, 3, 0, V)
         fetch(vector_gather, 1, 3, 0, V)
         round_fetched(3)
         fetch(vector_gather, 2, 0, 0, V)
         fetch(vector_gather, 3, 0, 0, V)
         fetch(scalar_gather, 2, 1, 0, V)
         fetch(scalar_gather, 3, 1, 0, V)
-        first_level_rounded(0)
-        first_level_rounded(1)
-        first_level(0, 1, 0, V)
+        first_level_rounded(0, 1, 1, 3)
+        first_level_rounded(0, 0, 0, 3)
+        first_level_rounded(1, 0, 1, 2)
+        first_level_rounded(1, 1, 0, 2)
+        first_level(0, 0, V)
 
         mean_t = [keep.tile([P, 2, P, 2], BF16, name="mean_t%d" % b, tag="mean_t%d" % b) for b in range(V // P)]
 
@@ -275,11 +300,12 @@ def tile_picked_pna_silu_e_kernel(
 
         fetch_last_lists(0, 2)
         fetch_last_lists(0, 3)
-        first_level(1, 1, 0, HALF_V)
+        first_level(1, 0, HALF_V)
         fetch_last_lists(1, 2)
+        fetch(scalar_gather, 2, 3, HALF_V, V)
         round_sum(0)
         round_sum(1)
-        fetch_last_lists(1, 3)
+        fetch(scalar_gather, 3, 3, HALF_V, V)
         first_mean = turn_back(4, 0, 2)
         round_sum(2)
         round_sum(3)
@@ -307,12 +333,13 @@ def tile_picked_pna_silu_e_kernel(
 
         def second_level(op, v0, v1):
             extreme = keep.tile([P, v1 - v0, 2, 2], BF16, name="extreme%d_%d" % (op == ALU.max, v0), align_bytes=64)
-            nc.vector.tensor_tensor(
-                out=extreme[:],
-                in0=pairs[0][op][:, :, v0:v1, :].rearrange("p u v e -> p v u e"),
-                in1=pairs[1][op][:, :, v0:v1, :].rearrange("p u v e -> p v u e"),
-                op=op,
-            )
+            half, first = divmod(v0, HALF_V)
+            sides = []
+            for c in range(2):
+                row0, row1 = (row_of(c, u, list(EXTREMES).index(op), half) for u in range(2))
+                rows = pairs[c][:, row0 : row1 + 1 : row1 - row0, first : first + v1 - v0, :]
+                sides.append(rows.rearrange("p u v e -> p v u e"))
+            nc.vector.tensor_tensor(out=extreme[:], in0=sides[0], in1=sides[1], op=op)
             return extreme[:].rearrange("p v u e -> p (v u e)")
 
         def store(v0, v1, copies, queues):
@@ -326,7 +353,7 @@ def tile_picked_pna_silu_e_kernel(
         smallest = second_level(ALU.min, 0, HALF_V)
         multiply(LARGEST, 0, HALF_V, largest)
         multiply(SMALLEST, 0, HALF_V, smallest)
-        first_level(1, 1, HALF_V, V)
+        first_level(1, HALF_V, V)
         multiply(MEAN, 0, HALF_V, first_mean[:])
         blocks = [(HALF_V + r * P, HALF_V + (r + 1) * P) for r in range(BLOCKS)]
         largest = second_level(ALU.max, HALF_V, V)

@@ -80,7 +80,7 @@ def tile_picked_pna_silu_e_kernel(
                     in_=scales_hbm[0, 4 * q : 4 * q + 4, :].bitcast(I32),
                 )
 
-        picked = [[keep.tile([P, 2, QUARTER_S], BF16, name="picked%d_%d" % (u, q)) for q in range(4)] for u in range(2)]
+        picked = [{q: keep.tile([P, 2, QUARTER_S], BF16, name="picked%d_%d" % (u, q)) for q in range(u, 4)} for u in range(2)]
         woven = [keep.tile([P, QUARTER_S, PACK], BF16, name="woven%d" % q, tag="woven%d" % q, align_bytes=64) for q in range(4)]
 
         def vector_gather(dst, window, offsets):
@@ -100,9 +100,9 @@ def tile_picked_pna_silu_e_kernel(
                 gather_x(vector_gather if q < 2 else scalar_gather, j, q)
         for q in range(4):
             weave(nc.vector.tensor_copy if q < 2 else nc.scalar.copy, 0, q)
-        for q in range(4):
-            gather_x(vector_gather if q < 3 else scalar_gather, 2, q)
-        nc.vector.tensor_copy(out=woven[0][:, :, 2], in_=picked[1][0][:, 0, :])
+        vector_gather(woven[0][:, :, 2], x_plane[2][:], entries(offs_sb, 0, QUARTER_S))
+        for q in range(1, 4):
+            gather_x(vector_gather if q < 2 else scalar_gather, 2, q)
         vector_gather(woven[0][:, :, 3], x_plane[3][:], entries(offs_sb, 0, QUARTER_S))
         for q in range(1, 4):
             gather_x(scalar_gather, 3, q)

from contextlib import ExitStack

import concourse.mybir as mybir
from concourse.masks import make_identity

K, T, S, V, H, N = 512, 2048, 1024, 512, 512, 256
FLOPS = 2 * K * H * S + 3 * 2 * H * N * V

F32 = mybir.dt.float32
BF16 = mybir.dt.bfloat16
I32 = mybir.dt.int32
U32 = mybir.dt.uint32
U16 = mybir.dt.uint16
U8 = mybir.dt.uint8
FP8X4 = mybir.dt.float8_e4m3fn_x4
FP4X4 = mybir.dt.float4_e2m1fn_x4
ACT = mybir.ActivationFunctionType
ALU = mybir.AluOpType

P = 128
PACK = 4
DEG = 4
PER_COLUMN = 16
HALF_S = S // 2
QUARTER_S = S // 4
HALF_V = V // 2
BLOCKS = HALF_V // P
MEAN, LARGEST, SMALLEST = 0, 1, 2


def tile_picked_pna_silu_e_kernel(
    tc, xT, w1, w2_words, w2_scales, w3_words, w3_scales, w4_words, w4_scales, offs, pos1, pos2, pos3, pos4, out
):
    nc = tc.nc
    with ExitStack() as ctx:
        lists = ctx.enter_context(tc.tile_pool(name="lists", bufs=1))
        keep = ctx.enter_context(tc.tile_pool(name="keep", bufs=1))
        psum = ctx.enter_context(tc.psum_pool(name="psum", bufs=1))

        def bank(n, shape):
            return psum.tile(shape, F32, name="bank%d" % n, tag="bank%d" % n)

        def entries(list_tile, c0, c1):
            return list_tile[:, c0 // PER_COLUMN : c1 // PER_COLUMN]

        zero_in = keep.tile([P, 1], F32, name="zero_in")
        zero_bias = keep.tile([P, 1], F32, name="zero_bias")
        nc.vector.memset(zero_in[:], 0.0)
        nc.scalar.activation(zero_bias[:], zero_in[:], ACT.Silu)
        ident = keep.tile([P, P], F32, name="ident")
        make_identity(nc, ident[:])
        wq_scales = keep.tile([P, 3 * N], U8, name="wq_scales", align_bytes=64)
        nc.gpsimd.memset(wq_scales[:], 0)

        x_rows = xT.rearrange("(p j) t -> p j t", j=PACK)
        x_plane = []
        offs_sb = lists.tile([P, S // PER_COLUMN], U16, name="offs_sb")
        for j in range(PACK):
            plane = keep.tile([P, T], F32, name="x_plane%d" % j)
            nc.sync.dma_start(out=plane[:], in_=x_rows[:, j, :])
            x_plane.append(plane)
            if j == 0:
                nc.sync.dma_start(offs_sb[:], offs)
        w_raw = keep.tile([P, PACK, H], F32, name="w_raw")
        nc.sync.dma_start(out=w_raw[:], in_=w1.rearrange("(p j) c -> p j c", j=PACK))
        pos_sb = []
        for d, pos in enumerate((pos1, pos2, pos3, pos4)):
            pos_tile = lists.tile([P, V // PER_COLUMN], U16, name="pos_sb%d" % d)
            nc.sync.dma_start(pos_tile[:], pos)
            pos_sb.append(pos_tile)
        wq_words = []
        for a, words_hbm in enumerate((w2_words, w3_words, w4_words)):
            words_tile = keep.tile([P, 2 * N], U8, name="wq_words%d" % a, align_bytes=64)
            nc.sync.dma_start(out=words_tile[:].bitcast(I32), in_=words_hbm[0].bitcast(I32))
            wq_words.append(words_tile)
        for a, scales_hbm in enumerate((w2_scales, w3_scales, w4_scales)):
            for q in range(4):
                nc.sync.dma_start(
                    out=wq_scales[32 * q : 32 * q + 4, a * N : (a + 1) * N].bitcast(I32),
                    in_=scales_hbm[0, 4 * q : 4 * q + 4, :].bitcast(I32),
                )

        picked = [{q: keep.tile([P, 2, QUARTER_S], BF16, name="picked%d_%d" % (u, q)) for q in range(u, 4)} for u in range(2)]
        woven = [keep.tile([P, QUARTER_S, PACK], BF16, name="woven%d" % q, tag="woven%d" % q, align_bytes=64) for q in range(4)]

        def vector_gather(dst, window, offsets):
            nc.vector.tensor_copy(out=dst, in_=window.indirect(offsets))

        def scalar_gather(dst, window, offsets):
            nc.scalar.activation(dst, window.indirect(offsets), ACT.Copy)

        def gather_x(gather, j, q):
            gather(picked[j // 2][q][:, j % 2, :], x_plane[j][:], entries(offs_sb, q * QUARTER_S, (q + 1) * QUARTER_S))

        def weave(copy, u, q, c0=0, c1=QUARTER_S):
            copy(out=woven[q][:, c0:c1, 2 * u : 2 * u + 2], in_=picked[u][q][:, :, c0:c1].rearrange("p e c -> p c e"))

        for j in range(2):
            for q in range(4):
                gather_x(vector_gather if q < 2 else scalar_gather, j, q)
        for q in range(4):
            weave(nc.vector.tensor_copy if q < 2 else nc.scalar.copy, 0, q)
        vector_gather(woven[0][:, :, 2], x_plane[2][:], entries(offs_sb, 0, QUARTER_S))
        for q in range(1, 4):
            gather_x(vector_gather if q < 2 else scalar_gather, 2, q)
        vector_gather(woven[0][:, :, 3], x_plane[3][:], entries(offs_sb, 0, QUARTER_S))
        for q in range(1, 4):
            gather_x(scalar_gather, 3, q)

        w_grouped = [keep.tile([P, 2, P, PACK], BF16, name="w_grouped0", tag="w_grouped0", align_bytes=64), None]
        x_codes = keep.tile([P, S], U32, name="x_codes", align_bytes=64)
        w_codes = keep.tile([P, H], U32, name="w_codes", align_bytes=64)
        w_scales = keep.tile([P, H], U8, name="w_scales", align_bytes=64)
        x_scales = {}

        def group_w(copy, g, m0, m1):
            copy(
                out=w_grouped[g][:, :, m0:m1, :].rearrange("p e m j -> p m j e"),
                in_=w_raw[:].rearrange("p j (m t) -> p m j t", t=PACK)[:, m0:m1, :, 2 * g : 2 * g + 2],
            )

        def quantize_w(t0, t1):
            nc.vector.quantize_mx(
                out=w_codes[:, t0 * P : t1 * P].bitcast(FP8X4),
                scales=w_scales[:, t0 * P : t1 * P],
                in_=w_grouped[t0 // 2][:, t0 % 2 : t0 % 2 + t1 - t0, :, :].rearrange("p e m j -> p (e m j)"),
            )

        def quantize_x(q):
            nc.vector.quantize_mx(
                out=x_codes[:, q * QUARTER_S : (q + 1) * QUARTER_S].bitcast(FP8X4),
                scales=x_scales[q],
                in_=woven[q][:].rearrange("p s j -> p (s j)"),
            )

        early_scales = keep.tile([P, S], U8, name="early_scales", align_bytes=64)
        for q in range(4):
            x_scales[q] = early_scales[:, q * QUARTER_S : (q + 1) * QUARTER_S]
        weave(nc.vector.tensor_copy, 1, 1)
        quantize_x(0)
        weave(nc.vector.tensor_copy, 1, 2)
        quantize_x(1)
        weave(nc.vector.tensor_copy, 1, 3)
        quantize_x(2)
        quantize_x(3)
        group_w(nc.scalar.copy, 0, 0, P)
        quantize_w(0, 1)
        quantize_w(1, 2)
        w_grouped[1] = keep.tile([P, 2, P, PACK], BF16, name="w_grouped_late", tag="w_grouped0", align_bytes=64)
        group_w(nc.vector.tensor_copy, 1, 0, P)
        quantize_w(2, 4)

        h = {}
        h_tags = ("h0", "h1", "h2", "fetched0_0_0")

        def h_stretch(bank_no, t, c0, c1):
            acc = bank(bank_no, [P, c1 - c0])
            for n0 in range(c0, c1, QUARTER_S):
                n1 = min(n0 + QUARTER_S, c1)
                nc.tensor.matmul_mx(
                    out=acc[:, n0 - c0 : n1 - c0],
                    lhsT=w_codes[:, t * P : (t + 1) * P].bitcast(FP8X4),
                    lhsT_scale=w_scales[:, t * P : (t + 1) * P],
                    rhs=x_codes[:, n0:n1].bitcast(FP8X4),
                    rhs_scale=early_scales[:, n0:n1],
                    start=True,
                    stop=True,
                )

            def silu():
                if t not in h:
                    h[t] = keep.tile([P, S], F32, name="h%d" % t, tag=h_tags[t], align_bytes=64)
                nc.scalar.activation(h[t][:, c0:c1], acc[:], ACT.Silu, bias=zero_bias[:])

            return silu

        for n, (c0, c1) in enumerate(((0, 128), (128, 384), (384, 640), (640, S))):
            h_stretch(4 + n, 0, c0, c1)()
        h_stretch(4, 1, 0, HALF_S)()
        h_stretch(5, 1, HALF_S, S)()
        late_silus = [h_stretch((6 + n) % 4 + 4, 2 + n // 2, n % 2 * HALF_S, (n % 2 + 1) * HALF_S) for n in range(4)]

        sum_t = [bank(b, [P, PACK, P]) for b in range(V // P)]
        opened = set()
        fetched = {}

        def fetch(gather, t, d, v0, v1, c0=None, c1=None):
            key = (d, t // 2, v0)
            if key == (DEG - 1, 1, 0) and key not in fetched:
                rows = keep.tile([P, 3, HALF_V], F32, name="fetched_last", align_bytes=64)
                fetched[key] = rows[:, 1:3, :]
                fetched[DEG - 1, 1, HALF_V] = rows[:, 0:2, :]
            if key not in fetched:
                tile = keep.tile([P, 2, v1 - v0], F32, name="fetched%d_%d_%d" % key, tag="fetched%d_%d_%d" % key, align_bytes=64)
                fetched[key] = tile[:]
            if c0 is None:
                c0, c1 = v0, v1
            dst = fetched[key][:, t % 2, :]
            gather(dst[:, c0 - v0 : c1 - v0], h[t][:], entries(pos_sb[d], c0, c1))
            for b in range(c0 // P, c1 // P):
                nc.tensor.matmul(
                    sum_t[b][:, t, :],
                    lhsT=dst[:, b * P - v0 : (b + 1) * P - v0],
                    rhs=ident[:],
                    is_transpose=True,
                    start=(b not in opened),
                    stop=(t == PACK - 1 and d == DEG - 1),
                )
                opened.add(b)

        pairs = {1: keep.tile([P, 8, HALF_V, 2], BF16, name="pairs1", align_bytes=64)}
        EXTREMES = (ALU.max, ALU.min)

        def row_of(c, u, n, half):
            if c == 1 and u == 1:
                return 4 + 2 * half + n
            return 4 * u + 2 * n + half

        def first_level(c, v0, v1):
            for n, op in enumerate(EXTREMES):
                row = row_of(c, 1, n, v0 // HALF_V)
                nc.vector.tensor_tensor(
                    out=pairs[c][:, row : row + (v1 - v0) // HALF_V, :, :].rearrange("p r v e -> p (r v) e"),
                    in0=fetched[2 * c, 1, v0].rearrange("p e v -> p v e"),
                    in1=fetched[2 * c + 1, 1, v0].rearrange("p e v -> p v e"),
                    op=op,
                )

        rounded = {}

        def round_fetched(d):
            if d == DEG - 1:
                pairs[0] = keep.tile([P, 8, HALF_V, 2], BF16, name="pairs0", tag="fetched2_0_0", align_bytes=64)
            c, row = ((1, 2), (1, 0), (1, 4), (0, 5))[d]
            rounded[d] = pairs[c][:, row : row + 2, :, :].rearrange("p r v e -> p (r v) e")
            if d == 0:
                for e in range(2):
                    nc.gpsimd.tensor_scalar(rounded[d][:, :, e], fetched[d, 0, 0][:, e, :], 1.0, 0.0, ALU.mult, ALU.add)
            else:
                nc.gpsimd.tensor_scalar(
                    rounded[d], fetched[d, 0, 0].rearrange("p e v -> p v e"), 1.0, 0.0, ALU.mult, ALU.add
                )

        def first_level_rounded(c, n, d0, d1):
            row = row_of(c, 0, n, 0)
            nc.vector.tensor_tensor(
                out=pairs[c][:, row : row + 2, :, :].rearrange("p r v e -> p (r v) e"),
                in0=rounded[d0],
                in1=rounded[d1],
                op=EXTREMES[n],
            )

        for d in range(2):
            fetch(vector_gather, 0, d, 0, V)
            fetch(scalar_gather, 1, d, 0, V)
            round_fetched(d)
        fetch(vector_gather, 0, 2, 0, V)
        fetch(scalar_gather, 1, 2, 0, V)
        fetch(vector_gather, 0, 3, 0, V)
        round_fetched(2)
        for silu in late_silus:
            silu()
        fetch(vector_gather, 1, 3, 0, V)
        round_fetched(3)
        fetch(vector_gather, 2, 0, 0, V)
        fetch(vector_gather, 3, 0, 0, V)
        fetch(scalar_gather, 2, 1, 0, V)
        fetch(scalar_gather, 3, 1, 0, V)
        first_level_rounded(0, 1, 1, 3)
        first_level_rounded(0, 0, 0, 3)
        first_level_rounded(1, 0, 1, 2)
        first_level_rounded(1, 1, 0, 2)
        first_level(0, 0, V)

        mean_t = [keep.tile([P, 2, P, 2], BF16, name="mean_t%d" % b, tag="mean_t%d" % b) for b in range(V // P)]

        def round_sum(b):
            nc.scalar.activation(
                mean_t[b][:], sum_t[b][:].rearrange("v (u e) p -> v u p e", e=2), ACT.Copy, scale=1.0 / DEG
            )

        def turn_back(bank_no, b0, b1):
            back = bank(bank_no, [P, 2, (b1 - b0) * P])
            for b in range(b0, b1):
                mean_words = mean_t[b][:].rearrange("v u p e -> v (u p e)").bitcast(F32)
                for u in range(2):
                    nc.tensor.transpose(
                        back[:, u, (b - b0) * P : (b - b0 + 1) * P], mean_words[:, u * P : (u + 1) * P], ident[:]
                    )
            mean = keep.tile([P, (b1 - b0) * P * PACK], BF16, name="mean%d" % b0, tag=h_tags[3] if b0 == 0 else "mean%d" % b0, align_bytes=64)
            nc.scalar.copy(
                out=mean[:].bitcast(F32).rearrange("p (v u) -> p v u", u=2),
                in_=back[:].rearrange("p u v -> p v u"),
            )
            return mean

        def fetch_last_lists(half, d):
            for t in range(2, PACK):
                fetch(scalar_gather, t, d, half * HALF_V, (half + 1) * HALF_V)

        fetch_last_lists(0, 2)
        fetch_last_lists(0, 3)
        first_level(1, 0, HALF_V)
        fetch_last_lists(1, 2)
        fetch(scalar_gather, 2, 3, HALF_V, V)
        round_sum(0)
        round_sum(1)
        fetch(scalar_gather, 3, 3, HALF_V, V)
        first_mean = turn_back(4, 0, 2)
        round_sum(2)
        round_sum(3)
        last_means = [turn_back(5, 2, 3), turn_back(4, 3, 4)]

        z_codes = [keep.tile([P, V], U32, name="z_codes%d" % a, align_bytes=64) for a in range(3)]
        z_scales = [keep.tile([P, V], U8, name="z_scales%d" % a, align_bytes=64) for a in range(3)]
        stretches = ((0, HALF_V, (6, 7)), (HALF_V, HALF_V + P, (0, 1)), (HALF_V + P, V, (2, 3)))
        res = {v0: [bank(n, [P, v1 - v0]) for n in banks] for v0, v1, banks in stretches}

        def multiply(a, c0, c1, z):
            nc.vector.quantize_mx(out=z_codes[a][:, c0:c1].bitcast(FP8X4), scales=z_scales[a][:, c0:c1], in_=z)
            for v0, v1, banks in stretches:
                if c0 <= v0 and v1 <= c1:
                    for m in range(N // P):
                        nc.tensor.matmul_mx(
                            out=res[v0][m][:],
                            lhsT=wq_words[a][:, m * 2 * P : (m + 1) * 2 * P].bitcast(FP4X4),
                            lhsT_scale=wq_scales[:, a * N + m * P : a * N + (m + 1) * P],
                            rhs=z_codes[a][:, v0:v1].bitcast(FP8X4),
                            rhs_scale=z_scales[a][:, v0:v1],
                            start=(a == LARGEST),
                            stop=(a == (SMALLEST if v0 == HALF_V else MEAN)),
                        )

        def second_level(op, v0, v1):
            extreme = keep.tile([P, v1 - v0, 2, 2], BF16, name="extreme%d_%d" % (op == ALU.max, v0), align_bytes=64)
            half, first = divmod(v0, HALF_V)
            sides = []
            for c in range(2):
                row0, row1 = (row_of(c, u, list(EXTREMES).index(op), half) for u in range(2))
                rows = pairs[c][:, row0 : row1 + 1 : row1 - row0, first : first + v1 - v0, :]
                sides.append(rows.rearrange("p u v e -> p v u e"))
            nc.vector.tensor_tensor(out=extreme[:], in0=sides[0], in1=sides[1], op=op)
            return extreme[:].rearrange("p v u e -> p (v u e)")

        def store(v0, v1, copies, queues):
            for m in range(N // P):
                tag = "mean_t%d" % (BLOCKS + 1 - m) if v0 == 0 else "staged%d_%d" % (m, v0)
                staged = keep.tile([P, v1 - v0], F32, name="staged%d_%d" % (m, v0), tag=tag)
                copies[m](out=staged[:], in_=res[v0][m][:])
                queues[m].dma_start(out=out[m * P : (m + 1) * P, v0:v1], in_=staged[:])

        largest = second_level(ALU.max, 0, HALF_V)
        smallest = second_level(ALU.min, 0, HALF_V)
        multiply(LARGEST, 0, HALF_V, largest)
        multiply(SMALLEST, 0, HALF_V, smallest)
        first_level(1, HALF_V, V)
        multiply(MEAN, 0, HALF_V, first_mean[:])
        blocks = [(HALF_V + r * P, HALF_V + (r + 1) * P) for r in range(BLOCKS)]
        largest = second_level(ALU.max, HALF_V, V)
        smallest = [second_level(ALU.min, *blocks[0])]
        multiply(LARGEST, HALF_V, V, largest)
        multiply(MEAN, *blocks[0], last_means[0][:])
        smallest.append(second_level(ALU.min, *blocks[1]))
        for r in range(BLOCKS):
            multiply(SMALLEST, *blocks[r], smallest[r])
        multiply(MEAN, *blocks[1], last_means[1][:])
        store(0, HALF_V, (nc.scalar.copy, nc.scalar.copy), (nc.sync, nc.sync))
        store(*blocks[0], (nc.scalar.copy, nc.vector.tensor_copy), (nc.sync, nc.sync))
        store(*blocks[1], (nc.vector.tensor_copy, nc.scalar.copy), (nc.sync, nc.scalar))
